import numpy as np
import ml_dtypes


def mxq(x, axis, fmt="e4m3"):
    dtype, down = {"e4m3": (ml_dtypes.float8_e4m3fn, 7), "e5m2": (ml_dtypes.float8_e5m2, 14)}[fmt]
    v = np.moveaxis(np.asarray(x, np.float32).astype(ml_dtypes.bfloat16).astype(np.float64), axis, -1)
    blocks = v.reshape(v.shape[:-1] + (-1, 32))
    amax = np.abs(blocks).max(-1, keepdims=True)
    byte = np.maximum(np.where(amax > 0, np.frexp(amax)[1] - 1 + 127, 0) - down, 1)
    scale = np.exp2(byte - 127.0)
    codes = (blocks / scale).astype(np.float32).astype(dtype).astype(np.float64)
    return np.moveaxis((codes * scale).reshape(v.shape), -1, axis)


WIDE = False


def mx_kscale(k):
    if not WIDE:
        return np.ones(k)
    levels = np.array([24, -24, 12, -12, 0])
    if k % 512:
        return np.exp2(np.random.permutation(np.resize(levels, k // 32))).repeat(32)
    a = np.empty((k // 512, 16))
    for p in range(k // 512):
        a[p, :8] = np.random.permutation(np.resize(levels, 8))
        for g in range(8):
            far = levels[np.abs(levels - a[p, g]) >= 10]
            a[p, g + 8] = far[np.random.randint(len(far))]
    return np.exp2(a.ravel()).repeat(32)


def f64(x):
    return np.asarray(x).astype(np.float64)


def striped(idx):
    return np.tile(idx.reshape(-1, 16).T, (8, 1)).astype(np.uint16)


def unstriped(offs):
    return offs[:16].T.reshape(-1).astype(np.int64)


E2M1 = np.array([0.0, 0.5, 1.0, 1.5, 2.0, 3.0, 4.0, 6.0, -0.0, -0.5, -1.0, -1.5, -2.0, -3.0, -4.0, -6.0])


def pack_weight(w, fmt):
    k, n = w.shape
    w = f64(np.asarray(w, np.float32).astype(ml_dtypes.bfloat16)).reshape(k // 32, 32, n)
    amax = np.abs(w).max(1)
    if fmt == "e4m3":
        byte = np.frexp(amax)[1] - 1 + 127 - 7
    else:
        mant, ex = np.frexp(amax / 6.0)
        byte = np.where(mant > 0.5, ex, ex - 1) + 127
    byte = np.clip(np.where(amax > 0, byte, 1), 1, 254)
    scaled = (w * np.exp2(127.0 - byte)[:, None, :]).reshape(k, n).astype(np.float32)
    by_word = np.ascontiguousarray(scaled.reshape(k // 512, 128, 4, n).transpose(0, 1, 3, 2))
    if fmt == "e4m3":
        words = by_word.astype(ml_dtypes.float8_e4m3fn).view(np.uint8)
    else:
        c = by_word.astype(ml_dtypes.float4_e2m1fn).view(np.uint8) & 0xF
        words = (c[..., 0::2] | (c[..., 1::2] << 4)).reshape(k // 512, 128, 2 * n)
    return np.ascontiguousarray(words), np.ascontiguousarray(byte.astype(np.uint8).reshape(k // 512, 16, n))


def unpack_weight(words, scales, fmt):
    g, _, n = scales.shape
    words = np.ascontiguousarray(words).reshape(g, 128, n, -1)
    if fmt == "e4m3":
        vals = words.view(ml_dtypes.float8_e4m3fn).astype(np.float64)
    else:
        nib = np.empty((g, 128, n, 4), np.uint8)
        nib[..., 0::2] = words & 0xF
        nib[..., 1::2] = words >> 4
        vals = E2M1[nib]
    vals = vals * np.repeat(np.exp2(scales.astype(np.float64) - 127.0), 8, axis=1)[..., None]
    return vals.transpose(0, 1, 3, 2).reshape(g * 512, n)


K, F, N, T, J = 512, 1024, 256, 4096, 1024


def setup_inputs():
    n = np.random.standard_normal
    s = mx_kscale(K)[:, None]
    u = mx_kscale(F)[:, None]
    p_tab = pack_weight(n((K, T)) * s, "e4m3")
    p_co = pack_weight(n((K, F)) / np.sqrt(K) / s, "e2m1")
    p_si = pack_weight(n((K, F)) / np.sqrt(K) / s, "e2m1")
    p_fb = pack_weight(np.abs(n((F, N))) / F / u, "e2m1")
    return {
        "tab_words": p_tab[0],
        "tab_scales": p_tab[1],
        "co_words": p_co[0],
        "co_scales": p_co[1],
        "si_words": p_si[0],
        "si_scales": p_si[1],
        "gn": (np.random.uniform(0.5, 2.0, F) * u[:, 0]).astype(np.float32),
        "fb_words": p_fb[0],
        "fb_scales": p_fb[1],
        "offs": striped(np.random.permutation(T)[:J]),
    }


def reference(tab_words, tab_scales, co_words, co_scales, si_words, si_scales, gn, fb_words, fb_scales, offs):
    idx = unstriped(offs)
    tab_ = unpack_weight(tab_words, tab_scales, "e4m3")[:, idx]
    co_ = unpack_weight(co_words, co_scales, "e2m1")
    si_ = unpack_weight(si_words, si_scales, "e2m1")
    re = co_.T @ tab_
    im = si_.T @ tab_
    h = f64(gn)[:, None] * ((re) ** 2 + (im) ** 2)
    h_ = mxq(h, 0, "e4m3")
    fb_ = unpack_weight(fb_words, fb_scales, "e2m1")
    y = fb_.T @ h_
    return np.sqrt(y)

@@ -1,0 +1,182 @@
+from contextlib import ExitStack
+
+import concourse.mybir as mybir
+
+K, F, N, T, J = 512, 1024, 256, 4096, 1024
+FLOPS = 2 * 2 * K * F * J + 2 * F * N * J
+
+F32 = mybir.dt.float32
+BF16 = mybir.dt.bfloat16
+I32 = mybir.dt.int32
+U32 = mybir.dt.uint32
+U16 = mybir.dt.uint16
+U8 = mybir.dt.uint8
+FP8X4 = mybir.dt.float8_e4m3fn_x4
+FP4X4 = mybir.dt.float4_e2m1fn_x4
+ADD = mybir.AluOpType.add
+MULT = mybir.AluOpType.mult
+SQUARE = mybir.ActivationFunctionType.Square
+SQRT = mybir.ActivationFunctionType.Sqrt
+
+P = 128
+PACK = 4
+PASSES = F // (P * PACK)
+BANK = 512
+HALF = J // 2
+CHUNKS = (256, 256, 256, 128, 128)
+VECTOR_UNITS = (0, 1, 2, 4, 5)
+RUN = 2
+
+
+def tile_list_meltab_root_kernel(
+    tc, tab_words, tab_scales, co_words, co_scales, si_words, si_scales, gn, fb_words, fb_scales, offs, out
+):
+    nc = tc.nc
+    with ExitStack() as ctx:
+        keep = ctx.enter_context(tc.tile_pool(name="keep", bufs=1))
+        work = ctx.enter_context(tc.tile_pool(name="work", bufs=3))
+        psum = ctx.enter_context(tc.psum_pool(name="psum", bufs=1))
+
+        offsets = keep.tile([P, J // 16], U16, name="offsets")
+        table = keep.tile([P, T], I32, name="table", align_bytes=64)
+        table_rows = keep.tile([P, T], U8, name="table_rows", tag="rows_then_si", align_bytes=64)
+        weight_rows = keep.tile([P, 2 * F], U8, name="weight_rows", tag="rows_then_co", align_bytes=64)
+        raw_co = keep.tile([P, 2 * F], U8, name="raw_co", tag="co_then_fb", align_bytes=64)
+        raw_si = keep.tile([P, 2 * F], U8, name="raw_si", align_bytes=64)
+        picked_rows = keep.tile([P, J], U8, name="picked_rows", tag="picked", align_bytes=64)
+        staged = keep.tile([P, 2 * F + J], U8, name="staged", tag="staged_then_fb", align_bytes=64)
+        planes = keep.tile([P, 2 * F + J], U8, name="planes", align_bytes=64)
+        gain = keep.tile([P, PASSES, PACK], F32, name="gain")
+        root_gain = keep.tile([P, PASSES, PACK], F32, name="root_gain")
+
+        nc.vector.memset(weight_rows[:].bitcast(I32), 0)
+        nc.vector.memset(table_rows[:].bitcast(I32), 0)
+        nc.vector.memset(planes[:].bitcast(I32), 0)
+
+        nc.sync.dma_start(offsets[:], offs)
+        nc.sync.dma_start(gain[:], gn.rearrange("(b p t) -> p b t", b=PASSES, t=PACK))
+        nc.sync.dma_start(raw_co[:].bitcast(I32), co_words[0].bitcast(I32))
+        nc.sync.dma_start(raw_si[:].bitcast(I32), si_words[0].bitcast(I32))
+        nc.sync.dma_start(table[:], tab_words[0].rearrange("p t i -> p (t i)").bitcast(I32))
+        nc.scalar.dma_start(weight_rows[0:P:8, 0:F].bitcast(I32), co_scales[0].bitcast(I32))
+        nc.scalar.dma_start(weight_rows[0:P:8, F : 2 * F].bitcast(I32), si_scales[0].bitcast(I32))
+        nc.scalar.dma_start(table_rows[0:P:8, :].bitcast(I32), tab_scales[0].bitcast(I32))
+
+        nc.scalar.activation(root_gain[:], gain[:], SQRT)
+
+        nc.vector.tensor_copy(
+            staged[:, 0 : 2 * F].rearrange("p (g t q) -> p g t q", t=PACK, q=P),
+            weight_rows[:].rearrange("p (g q t) -> p g t q", t=PACK, q=P),
+        )
+        nc.vector.tensor_copy(picked_rows[:], table_rows[:].indirect(offsets[:]))
+        nc.vector.tensor_copy(staged[:, 2 * F :].bitcast(I32), picked_rows[:].bitcast(I32))
+        for quad in range(4):
+            nc.scalar.dma_start(
+                planes[32 * quad : 32 * quad + 4, :].bitcast(I32),
+                staged[32 * quad : 32 * quad + 32 : 8, :].bitcast(I32),
+            )
+        dealt_co = keep.tile([P, 2 * F], U8, name="dealt_co", tag="rows_then_co", align_bytes=64)
+        dealt_si = keep.tile([P, 2 * F], U8, name="dealt_si", tag="rows_then_si", align_bytes=64)
+        for raw, dealt in ((raw_co, dealt_co), (raw_si, dealt_si)):
+            nc.vector.tensor_copy(
+                dealt[:].bitcast(U16).rearrange("p (b t q) -> p b t q", t=PACK, q=P),
+                raw[:].bitcast(U16).rearrange("p (b q t) -> p b t q", t=PACK, q=P),
+            )
+
+        picked = keep.tile([P, J], U32, name="picked", tag="picked", align_bytes=64)
+        fb_codes = keep.tile([P, PASSES, 2 * N], U8, name="fb_codes", tag="co_then_fb", align_bytes=64)
+        fb_plane = keep.tile([P, PASSES, N], U8, name="fb_plane", tag="staged_then_fb", align_bytes=64)
+
+        def load_filters():
+            nc.sync.dma_start(fb_codes[:].bitcast(I32), fb_words.rearrange("b p w -> p b w").bitcast(I32))
+            nc.vector.memset(fb_plane[:].bitcast(I32), 0)
+            for quad in range(4):
+                nc.sync.dma_start(
+                    fb_plane[32 * quad : 32 * quad + 4, :, :].bitcast(I32),
+                    fb_scales[:, 4 * quad : 4 * quad + 4, :].rearrange("b r n -> r b n").bitcast(I32),
+                )
+
+        def gather(h):
+            cols = HALF // 16
+            nc.vector.tensor_copy(picked[:, h * HALF : (h + 1) * HALF], table[:].bitcast(U32).indirect(offsets[:, h * cols : (h + 1) * cols]))
+
+        def first_stage(u, j0, width, b):
+            squares = work.tile([P, PACK, 2, width], F32, name="squares")
+            per_bank = BANK // (2 * width)
+            for t0 in range(0, PACK, per_bank):
+                bank = psum.tile([P, per_bank, 2, width], F32, name="bank", bufs=6)
+                for t in range(t0, t0 + per_bank):
+                    s = b * PACK + t
+                    for part, dealt in enumerate((dealt_co, dealt_si)):
+                        nc.tensor.matmul_mx(
+                            bank[:, t - t0, part, :],
+                            lhsT=dealt[:, 2 * P * s : 2 * P * (s + 1)].bitcast(FP4X4),
+                            lhsT_scale=planes[:, part * F + P * s : part * F + P * (s + 1)],
+                            rhs=picked[:, j0 : j0 + width].bitcast(FP8X4),
+                            rhs_scale=planes[:, 2 * F + j0 : 2 * F + j0 + width],
+                            start=True,
+                            stop=True,
+                        )
+                for t in range(t0, t0 + per_bank):
+                    sums = bank[:, t - t0, :, :].rearrange("p a c -> p (a c)")
+                    dst = squares[:, t, :, :].rearrange("p a c -> p (a c)")
+                    root = root_gain[:, b, t : t + 1]
+                    if t == 0 and u in VECTOR_UNITS:
+                        scaled = work.tile([P, 2 * width], F32, name="scaled", bufs=2)
+                        nc.vector.tensor_scalar(scaled[:], sums, root, None, MULT)
+                        nc.vector.tensor_tensor(dst, scaled[:], scaled[:], MULT)
+                    else:
+                        nc.scalar.activation(dst, sums, SQUARE, scale=root)
+            return squares
+
+        def power(squares, width):
+            woven = work.tile([P, width * PACK], BF16, name="woven", align_bytes=64, bufs=2)
+            nc.vector.tensor_tensor(
+                woven[:].rearrange("p (c i t) -> p c t i", i=RUN, t=PACK),
+                squares[:, :, 0, :].rearrange("p t (c i) -> p c t i", i=RUN),
+                squares[:, :, 1, :].rearrange("p t (c i) -> p c t i", i=RUN),
+                ADD,
+            )
+            codes = work.tile([P, width], U32, name="codes", align_bytes=64, bufs=4)
+            plane = work.tile([P, width], U8, name="plane", align_bytes=64, bufs=4)
+            nc.vector.quantize_mx(codes[:].bitcast(FP8X4), plane[:], woven[:])
+            return codes, plane
+
+        def second_stage(j0, width, quantised):
+            sums = psum.tile([P, N // P, width], F32, name="sums", bufs=2)
+            for a in range(N // P):
+                for c0 in range(0, width, P):
+                    for b, (codes, plane) in enumerate(quantised):
+                        nc.tensor.matmul_mx(
+                            sums[:, a, c0 : c0 + P],
+                            lhsT=fb_codes[:, b, 2 * P * a : 2 * P * (a + 1)].bitcast(FP4X4),
+                            lhsT_scale=fb_plane[:, b, P * a : P * (a + 1)],
+                            rhs=codes[:, c0 : c0 + P].bitcast(FP8X4),
+                            rhs_scale=plane[:, c0 : c0 + P],
+                            start=(b == 0),
+                            stop=(b == PASSES - 1),
+                        )
+            result = work.tile([P, N // P, width], F32, name="result")
+            nc.scalar.activation(result[:].rearrange("p a c -> p (a c)"), sums[:].rearrange("p a c -> p (a c)"), SQRT)
+            nc.sync.dma_start(out.rearrange("(a p) j -> p a j", p=P)[:, :, j0 : j0 + width], result[:])
+
+        units = []
+        j0 = 0
+        for width in CHUNKS:
+            for b in range(PASSES):
+                units.append((j0, width, b))
+            j0 = j0 + width
+
+        gather(0)
+        load_filters()
+        made = {}
+        quantised = {}
+        for u in range(len(units) + 2):
+            if u < len(units):
+                made[u] = first_stage(u, *units[u])
+            if u == 0:
+                gather(1)
+            if 1 <= u <= len(units):
+                quantised[u - 1] = power(made[u - 1], units[u - 1][1])
+            if u >= 2 and units[u - 2][2] == PASSES - 1:
+                second_stage(units[u - 2][0], units[u - 2][1], [quantised[u - 3], quantised[u - 2]])

@@ -39,66 +39,73 @@ def tile_list_meltab_root_kernel(
 
         offsets = keep.tile([P, J // 16], U16, name="offsets")
         table = keep.tile([P, T], I32, name="table", align_bytes=64)
-        table_rows = keep.tile([P, T], U8, name="table_rows", tag="rows_then_si", align_bytes=64)
-        weight_rows = keep.tile([P, 2 * F], U8, name="weight_rows", tag="rows_then_co", align_bytes=64)
-        raw_co = keep.tile([P, 2 * F], U8, name="raw_co", tag="co_then_fb", align_bytes=64)
-        raw_si = keep.tile([P, 2 * F], U8, name="raw_si", align_bytes=64)
-        picked_rows = keep.tile([P, J], U8, name="picked_rows", tag="picked", align_bytes=64)
-        staged = keep.tile([P, 2 * F + J], U8, name="staged", tag="staged_then_fb", align_bytes=64)
-        planes = keep.tile([P, 2 * F + J], U8, name="planes", align_bytes=64)
+        table_plane = keep.tile([P, T], U8, name="table_plane", tag="slot_d", align_bytes=64)
+        raw_co = keep.tile([P, 2 * F], U8, name="raw_co", tag="slot_b", align_bytes=64)
+        raw_si = keep.tile([P, 2 * F], U8, name="raw_si", tag="slot_c", align_bytes=64)
+        raw_co_plane = keep.tile([P, F], U8, name="raw_co_plane", tag="slot_a", align_bytes=64)
+        raw_si_plane = keep.tile([P, F], U8, name="raw_si_plane", tag="slot_e", align_bytes=64)
+        co_plane = keep.tile([P, F], U8, name="co_plane", align_bytes=64)
+        fb_codes = keep.tile([P, PASSES, 2 * N], U8, name="fb_codes", align_bytes=64)
+        fb_plane = keep.tile([P, PASSES, N], U8, name="fb_plane", align_bytes=64)
         gain = keep.tile([P, PASSES, PACK], F32, name="gain")
         root_gain = keep.tile([P, PASSES, PACK], F32, name="root_gain")
 
-        nc.vector.memset(weight_rows[:].bitcast(I32), 0)
-        nc.vector.memset(table_rows[:].bitcast(I32), 0)
-        nc.vector.memset(planes[:].bitcast(I32), 0)
+        nc.vector.memset(table_plane[:].bitcast(I32), 0)
+        nc.gpsimd.memset(raw_si_plane[:].bitcast(I32), 0)
+        nc.vector.memset(fb_plane[:].bitcast(I32), 0)
 
         nc.sync.dma_start(offsets[:], offs)
-        nc.sync.dma_start(gain[:], gn.rearrange("(b p t) -> p b t", b=PASSES, t=PACK))
+        for quad in range(4):
+            rows = co_scales[0, 4 * quad : 4 * quad + 4, :].bitcast(I32)
+            nc.sync.dma_start(
+                raw_co_plane[32 * quad : 32 * quad + 32, :].bitcast(I32),
+                rows.unsqueeze(0).to_broadcast([8, 4, F // 4]),
+            )
         nc.sync.dma_start(raw_co[:].bitcast(I32), co_words[0].bitcast(I32))
         nc.sync.dma_start(raw_si[:].bitcast(I32), si_words[0].bitcast(I32))
         nc.sync.dma_start(table[:], tab_words[0].rearrange("p t i -> p (t i)").bitcast(I32))
-        nc.scalar.dma_start(weight_rows[0:P:8, 0:F].bitcast(I32), co_scales[0].bitcast(I32))
-        nc.scalar.dma_start(weight_rows[0:P:8, F : 2 * F].bitcast(I32), si_scales[0].bitcast(I32))
-        nc.scalar.dma_start(table_rows[0:P:8, :].bitcast(I32), tab_scales[0].bitcast(I32))
+        nc.sync.dma_start(gain[:], gn.rearrange("(b p t) -> p b t", b=PASSES, t=PACK))
+        nc.sync.dma_start(fb_codes[:].bitcast(I32), fb_words.rearrange("b p w -> p b w").bitcast(I32))
+        for quad in range(4):
+            nc.scalar.dma_start(
+                table_plane[32 * quad : 32 * quad + 4, :].bitcast(I32),
+                tab_scales[0, 4 * quad : 4 * quad + 4, :].bitcast(I32),
+            )
+            nc.gpsimd.dma_start(
+                raw_si_plane[32 * quad : 32 * quad + 4, :].bitcast(I32),
+                si_scales[0, 4 * quad : 4 * quad + 4, :].bitcast(I32),
+            )
+        for quad in range(4):
+            nc.sync.dma_start(
+                fb_plane[32 * quad : 32 * quad + 4, :, :].bitcast(I32),
+                fb_scales[:, 4 * quad : 4 * quad + 4, :].rearrange("b r n -> r b n").bitcast(I32),
+            )
 
         nc.scalar.activation(root_gain[:], gain[:], SQRT)
 
-        nc.vector.tensor_copy(
-            staged[:, 0 : 2 * F].rearrange("p (g t q) -> p g t q", t=PACK, q=P),
-            weight_rows[:].rearrange("p (g q t) -> p g t q", t=PACK, q=P),
-        )
-        nc.vector.tensor_copy(picked_rows[:], table_rows[:].indirect(offsets[:]))
-        nc.vector.tensor_copy(staged[:, 2 * F :].bitcast(I32), picked_rows[:].bitcast(I32))
-        for quad in range(4):
-            nc.scalar.dma_start(
-                planes[32 * quad : 32 * quad + 4, :].bitcast(I32),
-                staged[32 * quad : 32 * quad + 32 : 8, :].bitcast(I32),
-            )
-        dealt_co = keep.tile([P, 2 * F], U8, name="dealt_co", tag="rows_then_co", align_bytes=64)
-        dealt_si = keep.tile([P, 2 * F], U8, name="dealt_si", tag="rows_then_si", align_bytes=64)
-        for raw, dealt in ((raw_co, dealt_co), (raw_si, dealt_si)):
+        def deal(dealt, raw):
             nc.vector.tensor_copy(
-                dealt[:].bitcast(U16).rearrange("p (b t q) -> p b t q", t=PACK, q=P),
-                raw[:].bitcast(U16).rearrange("p (b q t) -> p b t q", t=PACK, q=P),
+                dealt.rearrange("p (b t q) -> p b t q", t=PACK, q=P),
+                raw.rearrange("p (b q t) -> p b t q", t=PACK, q=P),
             )
 
-        picked = keep.tile([P, J], U32, name="picked", tag="picked", align_bytes=64)
-        fb_codes = keep.tile([P, PASSES, 2 * N], U8, name="fb_codes", tag="co_then_fb", align_bytes=64)
-        fb_plane = keep.tile([P, PASSES, N], U8, name="fb_plane", tag="staged_then_fb", align_bytes=64)
-
-        def load_filters():
-            nc.sync.dma_start(fb_codes[:].bitcast(I32), fb_words.rearrange("b p w -> p b w").bitcast(I32))
-            nc.vector.memset(fb_plane[:].bitcast(I32), 0)
-            for quad in range(4):
-                nc.sync.dma_start(
-                    fb_plane[32 * quad : 32 * quad + 4, :, :].bitcast(I32),
-                    fb_scales[:, 4 * quad : 4 * quad + 4, :].rearrange("b r n -> r b n").bitcast(I32),
-                )
+        deal(co_plane[:], raw_co_plane[:])
+        dealt_co = keep.tile([P, 2 * F], U8, name="dealt_co", tag="slot_a", align_bytes=64)
+        deal(dealt_co[:].bitcast(U16), raw_co[:].bitcast(U16))
+        dealt_si = keep.tile([P, 2 * F], U8, name="dealt_si", tag="slot_b", align_bytes=64)
+        deal(dealt_si[:].bitcast(U16), raw_si[:].bitcast(U16))
+        picked_plane = keep.tile([P, J], U8, name="picked_plane", tag="slot_c", align_bytes=64)
+        nc.vector.tensor_copy(picked_plane[:], table_plane[:].indirect(offsets[:]))
+        si_plane = keep.tile([P, F], U8, name="si_plane", tag="slot_d", align_bytes=64)
+        deal(si_plane[:], raw_si_plane[:])
+        picked = keep.tile([P, J], U32, name="picked", tag="slot_e", align_bytes=64)
 
         def gather(h):
             cols = HALF // 16
-            nc.vector.tensor_copy(picked[:, h * HALF : (h + 1) * HALF], table[:].bitcast(U32).indirect(offsets[:, h * cols : (h + 1) * cols]))
+            nc.vector.tensor_copy(
+                picked[:, h * HALF : (h + 1) * HALF],
+                table[:].bitcast(U32).indirect(offsets[:, h * cols : (h + 1) * cols]),
+            )
 
         def first_stage(u, j0, width, b):
             squares = work.tile([P, PACK, 2, width], F32, name="squares")
@@ -107,13 +114,13 @@ def tile_list_meltab_root_kernel(
                 bank = psum.tile([P, per_bank, 2, width], F32, name="bank", bufs=6)
                 for t in range(t0, t0 + per_bank):
                     s = b * PACK + t
-                    for part, dealt in enumerate((dealt_co, dealt_si)):
+                    for part, (dealt, plane) in enumerate(((dealt_co, co_plane), (dealt_si, si_plane))):
                         nc.tensor.matmul_mx(
                             bank[:, t - t0, part, :],
                             lhsT=dealt[:, 2 * P * s : 2 * P * (s + 1)].bitcast(FP4X4),
-                            lhsT_scale=planes[:, part * F + P * s : part * F + P * (s + 1)],
+                            lhsT_scale=plane[:, P * s : P * (s + 1)],
                             rhs=picked[:, j0 : j0 + width].bitcast(FP8X4),
-                            rhs_scale=planes[:, 2 * F + j0 : 2 * F + j0 + width],
+                            rhs_scale=picked_plane[:, j0 : j0 + width],
                             start=True,
                             stop=True,
                         )
@@ -168,7 +175,6 @@ def tile_list_meltab_root_kernel(
             j0 = j0 + width
 
         gather(0)
-        load_filters()
         made = {}
         quantised = {}
         for u in range(len(units) + 2):

@@ -39,88 +39,92 @@ def tile_list_meltab_root_kernel(
 
         offsets = keep.tile([P, J // 16], U16, name="offsets")
         table = keep.tile([P, T], I32, name="table", align_bytes=64)
-        table_plane = keep.tile([P, T], U8, name="table_plane", tag="slot_d", align_bytes=64)
-        raw_co = keep.tile([P, 2 * F], U8, name="raw_co", tag="slot_b", align_bytes=64)
-        raw_si = keep.tile([P, 2 * F], U8, name="raw_si", tag="slot_c", align_bytes=64)
-        raw_co_plane = keep.tile([P, F], U8, name="raw_co_plane", tag="slot_a", align_bytes=64)
-        raw_si_plane = keep.tile([P, F], U8, name="raw_si_plane", tag="slot_e", align_bytes=64)
-        co_plane = keep.tile([P, F], U8, name="co_plane", align_bytes=64)
-        fb_codes = keep.tile([P, PASSES, 2 * N], U8, name="fb_codes", align_bytes=64)
-        fb_plane = keep.tile([P, PASSES, N], U8, name="fb_plane", align_bytes=64)
+        table_rows = keep.tile([P, T], U8, name="table_rows", align_bytes=64)
+        weight_rows = keep.tile([P, F], U8, name="weight_rows", align_bytes=64)
+        raw_co = keep.tile([P, 2 * F], U8, name="raw_co", align_bytes=64)
+        raw_si = keep.tile([P, 2 * F], U8, name="raw_si", align_bytes=64)
+        dealt_co = keep.tile([P, 2 * F], U8, name="dealt_co", align_bytes=64)
+        dealt_si = keep.tile([P, 2 * F], U8, name="dealt_si", align_bytes=64)
+        picked_rows = keep.tile([P, J], U8, name="picked_rows", align_bytes=64)
+        picked = keep.tile([P, J], U32, name="picked", align_bytes=64)
+        early_rows = keep.tile([P, F + HALF], U8, name="early_rows", tag="rows_then_fb", align_bytes=64)
+        late_rows = keep.tile([P, HALF + PASSES * N], U8, name="late_rows", align_bytes=64)
+        early_planes = keep.tile([P, 2 * (F + HALF)], U8, name="early_planes", align_bytes=64)
+        late_planes = keep.tile([P, HALF + PASSES * N], U8, name="late_planes", align_bytes=64)
         gain = keep.tile([P, PASSES, PACK], F32, name="gain")
         root_gain = keep.tile([P, PASSES, PACK], F32, name="root_gain")
 
-        nc.vector.memset(table_plane[:].bitcast(I32), 0)
-        nc.gpsimd.memset(raw_si_plane[:].bitcast(I32), 0)
-        nc.vector.memset(fb_plane[:].bitcast(I32), 0)
+        nc.vector.memset(weight_rows[:].bitcast(I32), 0)
+        nc.vector.memset(table_rows[:, 0 : T // 2].bitcast(I32), 0)
+        nc.gpsimd.memset(table_rows[:, T // 2 :].bitcast(I32), 0)
+        nc.gpsimd.memset(early_planes[:].bitcast(I32), 0)
+        nc.gpsimd.memset(late_planes[:].bitcast(I32), 0)
 
         nc.sync.dma_start(offsets[:], offs)
-        for quad in range(4):
-            rows = co_scales[0, 4 * quad : 4 * quad + 4, :].bitcast(I32)
-            nc.sync.dma_start(
-                raw_co_plane[32 * quad : 32 * quad + 32, :].bitcast(I32),
-                rows.unsqueeze(0).to_broadcast([8, 4, F // 4]),
-            )
         nc.sync.dma_start(raw_co[:].bitcast(I32), co_words[0].bitcast(I32))
         nc.sync.dma_start(raw_si[:].bitcast(I32), si_words[0].bitcast(I32))
-        nc.sync.dma_start(table[:], tab_words[0].rearrange("p t i -> p (t i)").bitcast(I32))
         nc.sync.dma_start(gain[:], gn.rearrange("(b p t) -> p b t", b=PASSES, t=PACK))
-        nc.sync.dma_start(fb_codes[:].bitcast(I32), fb_words.rearrange("b p w -> p b w").bitcast(I32))
-        for quad in range(4):
-            nc.scalar.dma_start(
-                table_plane[32 * quad : 32 * quad + 4, :].bitcast(I32),
-                tab_scales[0, 4 * quad : 4 * quad + 4, :].bitcast(I32),
-            )
-            nc.gpsimd.dma_start(
-                raw_si_plane[32 * quad : 32 * quad + 4, :].bitcast(I32),
-                si_scales[0, 4 * quad : 4 * quad + 4, :].bitcast(I32),
-            )
-        for quad in range(4):
-            nc.sync.dma_start(
-                fb_plane[32 * quad : 32 * quad + 4, :, :].bitcast(I32),
-                fb_scales[:, 4 * quad : 4 * quad + 4, :].rearrange("b r n -> r b n").bitcast(I32),
-            )
+        nc.sync.dma_start(weight_rows[0:P:8, :].bitcast(I32), co_scales[0].bitcast(I32))
+        nc.sync.dma_start(weight_rows[4:P:8, :].bitcast(I32), si_scales[0].bitcast(I32))
+        nc.sync.dma_start(table_rows[0:P:8, :].bitcast(I32), tab_scales[0].bitcast(I32))
+        nc.sync.dma_start(table[:], tab_words[0].rearrange("p t i -> p (t i)").bitcast(I32))
+        nc.sync.dma_start(
+            late_rows[0:P:8, HALF:].rearrange("q (b n) -> q b n", b=PASSES).bitcast(I32),
+            fb_scales.rearrange("b q n -> q b n").bitcast(I32),
+        )
 
         nc.scalar.activation(root_gain[:], gain[:], SQRT)
 
         def deal(dealt, raw):
             nc.vector.tensor_copy(
-                dealt.rearrange("p (b t q) -> p b t q", t=PACK, q=P),
-                raw.rearrange("p (b q t) -> p b t q", t=PACK, q=P),
+                dealt.rearrange("p (g t q) -> p g t q", t=PACK, q=P),
+                raw.rearrange("p (g q t) -> p g t q", t=PACK, q=P),
             )
 
-        deal(co_plane[:], raw_co_plane[:])
-        dealt_co = keep.tile([P, 2 * F], U8, name="dealt_co", tag="slot_a", align_bytes=64)
-        deal(dealt_co[:].bitcast(U16), raw_co[:].bitcast(U16))
-        dealt_si = keep.tile([P, 2 * F], U8, name="dealt_si", tag="slot_b", align_bytes=64)
-        deal(dealt_si[:].bitcast(U16), raw_si[:].bitcast(U16))
-        picked_plane = keep.tile([P, J], U8, name="picked_plane", tag="slot_c", align_bytes=64)
-        nc.vector.tensor_copy(picked_plane[:], table_plane[:].indirect(offsets[:]))
-        si_plane = keep.tile([P, F], U8, name="si_plane", tag="slot_d", align_bytes=64)
-        deal(si_plane[:], raw_si_plane[:])
-        picked = keep.tile([P, J], U32, name="picked", tag="slot_e", align_bytes=64)
+        def half_list(h):
+            return offsets[:, h * (HALF // 16) : (h + 1) * (HALF // 16)]
+
+        def gather_scales(h):
+            nc.vector.tensor_copy(picked_rows[:, h * HALF : (h + 1) * HALF], table_rows[:].indirect(half_list(h)))
 
         def gather(h):
-            cols = HALF // 16
-            nc.vector.tensor_copy(
-                picked[:, h * HALF : (h + 1) * HALF],
-                table[:].bitcast(U32).indirect(offsets[:, h * cols : (h + 1) * cols]),
-            )
+            nc.vector.tensor_copy(picked[:, h * HALF : (h + 1) * HALF], table[:].bitcast(U32).indirect(half_list(h)))
+
+        def place(queue, planes, rows, step):
+            for quad in range(4):
+                queue.dma_start(
+                    planes[32 * quad : 32 * quad + 4, :].bitcast(I32),
+                    rows[32 * quad : 32 * quad + 32 : step, :].bitcast(I32),
+                )
+
+        deal(early_rows[:, 0:F], weight_rows[:])
+        gather_scales(0)
+        nc.vector.tensor_copy(early_rows[:, F:].bitcast(I32), picked_rows[:, 0:HALF].bitcast(I32))
+        place(nc.scalar, early_planes, early_rows, 4)
+        deal(dealt_co[:].bitcast(U16), raw_co[:].bitcast(U16))
+        deal(dealt_si[:].bitcast(U16), raw_si[:].bitcast(U16))
+        fb_codes = keep.tile([P, PASSES, 2 * N], U8, name="fb_codes", tag="rows_then_fb", align_bytes=64)
+        nc.sync.dma_start(fb_codes[:].bitcast(I32), fb_words.rearrange("b p w -> p b w").bitcast(I32))
+        gather_scales(1)
+        nc.vector.tensor_copy(late_rows[:, 0:HALF].bitcast(I32), picked_rows[:, HALF:].bitcast(I32))
+        picked_planes = (early_planes[:, F : F + HALF], late_planes[:, 0:HALF])
+        fb_plane = late_planes[:, HALF:].rearrange("p (b n) -> p b n", b=PASSES)
 
         def first_stage(u, j0, width, b):
             squares = work.tile([P, PACK, 2, width], F32, name="squares")
             per_bank = BANK // (2 * width)
+            h, c0 = divmod(j0, HALF)
             for t0 in range(0, PACK, per_bank):
                 bank = psum.tile([P, per_bank, 2, width], F32, name="bank", bufs=6)
                 for t in range(t0, t0 + per_bank):
                     s = b * PACK + t
-                    for part, (dealt, plane) in enumerate(((dealt_co, co_plane), (dealt_si, si_plane))):
+                    for part, dealt in enumerate((dealt_co, dealt_si)):
                         nc.tensor.matmul_mx(
                             bank[:, t - t0, part, :],
                             lhsT=dealt[:, 2 * P * s : 2 * P * (s + 1)].bitcast(FP4X4),
-                            lhsT_scale=plane[:, P * s : P * (s + 1)],
+                            lhsT_scale=early_planes[:, part * (F + HALF) + P * s : part * (F + HALF) + P * (s + 1)],
                             rhs=picked[:, j0 : j0 + width].bitcast(FP8X4),
-                            rhs_scale=picked_plane[:, j0 : j0 + width],
+                            rhs_scale=picked_planes[h][:, c0 : c0 + width],
                             start=True,
                             stop=True,
                         )
@@ -149,20 +153,20 @@ def tile_list_meltab_root_kernel(
             nc.vector.quantize_mx(codes[:].bitcast(FP8X4), plane[:], woven[:])
             return codes, plane
 
-        def second_stage(j0, width, quantised):
-            sums = psum.tile([P, N // P, width], F32, name="sums", bufs=2)
+        def second_stage(sums, width, b, codes, plane):
             for a in range(N // P):
                 for c0 in range(0, width, P):
-                    for b, (codes, plane) in enumerate(quantised):
-                        nc.tensor.matmul_mx(
-                            sums[:, a, c0 : c0 + P],
-                            lhsT=fb_codes[:, b, 2 * P * a : 2 * P * (a + 1)].bitcast(FP4X4),
-                            lhsT_scale=fb_plane[:, b, P * a : P * (a + 1)],
-                            rhs=codes[:, c0 : c0 + P].bitcast(FP8X4),
-                            rhs_scale=plane[:, c0 : c0 + P],
-                            start=(b == 0),
-                            stop=(b == PASSES - 1),
-                        )
+                    nc.tensor.matmul_mx(
+                        sums[:, a, c0 : c0 + P],
+                        lhsT=fb_codes[:, b, 2 * P * a : 2 * P * (a + 1)].bitcast(FP4X4),
+                        lhsT_scale=fb_plane[:, b, P * a : P * (a + 1)],
+                        rhs=codes[:, c0 : c0 + P].bitcast(FP8X4),
+                        rhs_scale=plane[:, c0 : c0 + P],
+                        start=(b == 0 and a == 0 and c0 == 0),
+                        stop=(b == PASSES - 1 and a == N // P - 1 and c0 == width - P),
+                    )
+
+        def finish(sums, j0, width):
             result = work.tile([P, N // P, width], F32, name="result")
             nc.scalar.activation(result[:].rearrange("p a c -> p (a c)"), sums[:].rearrange("p a c -> p (a c)"), SQRT)
             nc.sync.dma_start(out.rearrange("(a p) j -> p a j", p=P)[:, :, j0 : j0 + width], result[:])
@@ -175,6 +179,7 @@ def tile_list_meltab_root_kernel(
             j0 = j0 + width
 
         gather(0)
+        place(nc.sync, late_planes, late_rows, 8)
         made = {}
         quantised = {}
         for u in range(len(units) + 2):
@@ -184,5 +189,10 @@ def tile_list_meltab_root_kernel(
                 gather(1)
             if 1 <= u <= len(units):
                 quantised[u - 1] = power(made[u - 1], units[u - 1][1])
-            if u >= 2 and units[u - 2][2] == PASSES - 1:
-                second_stage(units[u - 2][0], units[u - 2][1], [quantised[u - 3], quantised[u - 2]])
+            if u >= 2:
+                j0, width, b = units[u - 2]
+                if b == 0:
+                    sums = psum.tile([P, N // P, width], F32, name="sums", bufs=2)
+                second_stage(sums, width, b, *quantised[u - 2])
+                if b == PASSES - 1:
+                    finish(sums, j0, width)

@@ -57,8 +57,8 @@ def tile_list_meltab_root_kernel(
         nc.vector.memset(weight_rows[:].bitcast(I32), 0)
         nc.vector.memset(table_rows[:, 0 : T // 2].bitcast(I32), 0)
         nc.gpsimd.memset(table_rows[:, T // 2 :].bitcast(I32), 0)
-        nc.gpsimd.memset(early_planes[:].bitcast(I32), 0)
-        nc.gpsimd.memset(late_planes[:].bitcast(I32), 0)
+        nc.vector.memset(early_planes[:].bitcast(I32), 0)
+        nc.vector.memset(late_planes[:].bitcast(I32), 0)
 
         nc.sync.dma_start(offsets[:], offs)
         nc.sync.dma_start(raw_co[:].bitcast(I32), co_words[0].bitcast(I32))
@@ -111,9 +111,10 @@ def tile_list_meltab_root_kernel(
         fb_plane = late_planes[:, HALF:].rearrange("p (b n) -> p b n", b=PASSES)
 
         def first_stage(u, j0, width, b):
-            squares = work.tile([P, PACK, 2, width], F32, name="squares")
+            squares = work.tile([P, PACK, 2, width], F32, name="squares", bufs=3)
             per_bank = BANK // (2 * width)
             h, c0 = divmod(j0, HALF)
+            scaled = None
             for t0 in range(0, PACK, per_bank):
                 bank = psum.tile([P, per_bank, 2, width], F32, name="bank", bufs=6)
                 for t in range(t0, t0 + per_bank):
@@ -130,26 +131,30 @@ def tile_list_meltab_root_kernel(
                         )
                 for t in range(t0, t0 + per_bank):
                     sums = bank[:, t - t0, :, :].rearrange("p a c -> p (a c)")
-                    dst = squares[:, t, :, :].rearrange("p a c -> p (a c)")
                     root = root_gain[:, b, t : t + 1]
                     if t == 0 and u in VECTOR_UNITS:
                         scaled = work.tile([P, 2 * width], F32, name="scaled", bufs=2)
                         nc.vector.tensor_scalar(scaled[:], sums, root, None, MULT)
-                        nc.vector.tensor_tensor(dst, scaled[:], scaled[:], MULT)
                     else:
-                        nc.scalar.activation(dst, sums, SQUARE, scale=root)
-            return squares
+                        nc.scalar.activation(squares[:, t, :, :].rearrange("p a c -> p (a c)"), sums, SQUARE, scale=root)
+            return squares, scaled
+
+        def square_on_vector(squares, scaled):
+            nc.vector.tensor_tensor(squares[:, 0, :, :].rearrange("p a c -> p (a c)"), scaled[:], scaled[:], MULT)
 
         def power(squares, width):
-            woven = work.tile([P, width * PACK], BF16, name="woven", align_bytes=64, bufs=2)
+            woven = work.tile([P, width * PACK], BF16, name="woven", align_bytes=64, bufs=3)
             nc.vector.tensor_tensor(
                 woven[:].rearrange("p (c i t) -> p c t i", i=RUN, t=PACK),
                 squares[:, :, 0, :].rearrange("p t (c i) -> p c t i", i=RUN),
                 squares[:, :, 1, :].rearrange("p t (c i) -> p c t i", i=RUN),
                 ADD,
             )
-            codes = work.tile([P, width], U32, name="codes", align_bytes=64, bufs=4)
-            plane = work.tile([P, width], U8, name="plane", align_bytes=64, bufs=4)
+            return woven
+
+        def quantise(woven, width):
+            codes = work.tile([P, width], U32, name="codes", align_bytes=64)
+            plane = work.tile([P, width], U8, name="plane", align_bytes=64)
             nc.vector.quantize_mx(codes[:].bitcast(FP8X4), plane[:], woven[:])
             return codes, plane
 
@@ -181,18 +186,25 @@ def tile_list_meltab_root_kernel(
         gather(0)
         place(nc.sync, late_planes, late_rows, 8)
         made = {}
+        powers = {}
         quantised = {}
-        for u in range(len(units) + 2):
-            if u < len(units):
+        sums = {}
+        count = len(units)
+        for u in range(count + 4):
+            if u < count:
                 made[u] = first_stage(u, *units[u])
+            if 1 <= u <= count:
+                powers[u - 1] = power(made[u - 1][0], units[u - 1][1])
             if u == 0:
                 gather(1)
-            if 1 <= u <= len(units):
-                quantised[u - 1] = power(made[u - 1], units[u - 1][1])
-            if u >= 2:
-                j0, width, b = units[u - 2]
+            if u in VECTOR_UNITS:
+                square_on_vector(*made[u])
+            if 2 <= u <= count + 1:
+                quantised[u - 2] = quantise(powers[u - 2], units[u - 2][1])
+            if 4 <= u and units[u - 4][2] == PASSES - 1:
+                finish(sums[units[u - 4][0]], units[u - 4][0], units[u - 4][1])
+            if 3 <= u <= count + 2:
+                j0, width, b = units[u - 3]
                 if b == 0:
-                    sums = psum.tile([P, N // P, width], F32, name="sums", bufs=2)
-                second_stage(sums, width, b, *quantised[u - 2])
-                if b == PASSES - 1:
-                    finish(sums, j0, width)
+                    sums[j0] = psum.tile([P, N // P, width], F32, name="sums", bufs=2)
+                second_stage(sums[j0], width, b, *quantised[u - 3])

@@ -25,7 +25,7 @@ BANK = 512
 HALF = J // 2
 CHUNKS = (256, 256, 256, 128, 128)
 VECTOR_UNITS = (0, 1, 2, 4, 5)
-RUN = 2
+RUN = 4
 
 
 def tile_list_meltab_root_kernel(

@@ -100,7 +100,7 @@ def tile_list_meltab_root_kernel(
         deal(early_rows[:, 0:F], weight_rows[:])
         gather_scales(0)
         nc.vector.tensor_copy(early_rows[:, F:].bitcast(I32), picked_rows[:, 0:HALF].bitcast(I32))
-        place(nc.scalar, early_planes, early_rows, 4)
+        place(nc.sync, early_planes, early_rows, 4)
         deal(dealt_co[:].bitcast(U16), raw_co[:].bitcast(U16))
         deal(dealt_si[:].bitcast(U16), raw_si[:].bitcast(U16))
         fb_codes = keep.tile([P, PASSES, 2 * N], U8, name="fb_codes", tag="rows_then_fb", align_bytes=64)

@@ -26,6 +26,9 @@ HALF = J // 2
 CHUNKS = (256, 256, 256, 128, 128)
 VECTOR_UNITS = (0, 1, 2, 4, 5)
 RUN = 4
+GROUP = P * PACK
+EARLY = GROUP + HALF
+LATE = GROUP + HALF + N
 
 
 def tile_list_meltab_root_kernel(
@@ -47,10 +50,10 @@ def tile_list_meltab_root_kernel(
         dealt_si = keep.tile([P, 2 * F], U8, name="dealt_si", align_bytes=64)
         picked_rows = keep.tile([P, J], U8, name="picked_rows", align_bytes=64)
         picked = keep.tile([P, J], U32, name="picked", align_bytes=64)
-        early_rows = keep.tile([P, F + HALF], U8, name="early_rows", tag="rows_then_fb", align_bytes=64)
-        late_rows = keep.tile([P, HALF + PASSES * N], U8, name="late_rows", align_bytes=64)
-        early_planes = keep.tile([P, 2 * (F + HALF)], U8, name="early_planes", align_bytes=64)
-        late_planes = keep.tile([P, HALF + PASSES * N], U8, name="late_planes", align_bytes=64)
+        early_rows = keep.tile([P, EARLY], U8, name="early_rows", tag="rows_then_fb", align_bytes=64)
+        late_rows = keep.tile([P, LATE], U8, name="late_rows", align_bytes=64)
+        early_planes = keep.tile([P, 2 * EARLY], U8, name="early_planes", align_bytes=64)
+        late_planes = keep.tile([P, 2 * LATE], U8, name="late_planes", align_bytes=64)
         gain = keep.tile([P, PASSES, PACK], F32, name="gain")
         root_gain = keep.tile([P, PASSES, PACK], F32, name="root_gain")
 
@@ -69,7 +72,7 @@ def tile_list_meltab_root_kernel(
         nc.sync.dma_start(table_rows[0:P:8, :].bitcast(I32), tab_scales[0].bitcast(I32))
         nc.sync.dma_start(table[:], tab_words[0].rearrange("p t i -> p (t i)").bitcast(I32))
         nc.sync.dma_start(
-            late_rows[0:P:8, HALF:].rearrange("q (b n) -> q b n", b=PASSES).bitcast(I32),
+            late_rows[0:P:4, GROUP + HALF :].bitcast(I32),
             fb_scales.rearrange("b q n -> q b n").bitcast(I32),
         )
 
@@ -97,18 +100,20 @@ def tile_list_meltab_root_kernel(
                     rows[32 * quad : 32 * quad + 32 : step, :].bitcast(I32),
                 )
 
-        deal(early_rows[:, 0:F], weight_rows[:])
+        deal(early_rows[:, 0:GROUP], weight_rows[:, 0:GROUP])
         gather_scales(0)
-        nc.vector.tensor_copy(early_rows[:, F:].bitcast(I32), picked_rows[:, 0:HALF].bitcast(I32))
+        nc.vector.tensor_copy(early_rows[:, GROUP:].bitcast(I32), picked_rows[:, 0:HALF].bitcast(I32))
         place(nc.sync, early_planes, early_rows, 4)
         deal(dealt_co[:].bitcast(U16), raw_co[:].bitcast(U16))
         deal(dealt_si[:].bitcast(U16), raw_si[:].bitcast(U16))
         fb_codes = keep.tile([P, PASSES, 2 * N], U8, name="fb_codes", tag="rows_then_fb", align_bytes=64)
-        nc.sync.dma_start(fb_codes[:].bitcast(I32), fb_words.rearrange("b p w -> p b w").bitcast(I32))
+        nc.scalar.dma_start(fb_codes[:].bitcast(I32), fb_words.rearrange("b p w -> p b w").bitcast(I32))
+        deal(late_rows[:, 0:GROUP], weight_rows[:, GROUP:])
         gather_scales(1)
-        nc.vector.tensor_copy(late_rows[:, 0:HALF].bitcast(I32), picked_rows[:, HALF:].bitcast(I32))
-        picked_planes = (early_planes[:, F : F + HALF], late_planes[:, 0:HALF])
-        fb_plane = late_planes[:, HALF:].rearrange("p (b n) -> p b n", b=PASSES)
+        nc.vector.tensor_copy(late_rows[:, GROUP : GROUP + HALF].bitcast(I32), picked_rows[:, HALF:].bitcast(I32))
+        planes = (early_planes[:].rearrange("p (a w) -> p a w", a=2), late_planes[:].rearrange("p (a w) -> p a w", a=2))
+        picked_planes = [plane[:, 0, GROUP : GROUP + HALF] for plane in planes]
+        fb_plane = planes[1][:, :, GROUP + HALF :]
 
         def first_stage(u, j0, width, b):
             squares = work.tile([P, PACK, 2, width], F32, name="squares", bufs=3)
@@ -123,7 +128,7 @@ def tile_list_meltab_root_kernel(
                         nc.tensor.matmul_mx(
                             bank[:, t - t0, part, :],
                             lhsT=dealt[:, 2 * P * s : 2 * P * (s + 1)].bitcast(FP4X4),
-                            lhsT_scale=early_planes[:, part * (F + HALF) + P * s : part * (F + HALF) + P * (s + 1)],
+                            lhsT_scale=planes[b][:, part, P * t : P * (t + 1)],
                             rhs=picked[:, j0 : j0 + width].bitcast(FP8X4),
                             rhs_scale=picked_planes[h][:, c0 : c0 + width],
                             start=True,
@@ -183,8 +188,10 @@ def tile_list_meltab_root_kernel(
                 units.append((j0, width, b))
             j0 = j0 + width
 
+        units[1], units[2] = units[2], units[1]
+
         gather(0)
-        place(nc.sync, late_planes, late_rows, 8)
+        place(nc.sync, late_planes, late_rows, 4)
         made = {}
         powers = {}
         quantised = {}

@@ -23,8 +23,17 @@ PACK = 4
 PASSES = F // (P * PACK)
 BANK = 512
 HALF = J // 2
-CHUNKS = (256, 256, 256, 128, 128)
-VECTOR_UNITS = (0, 1, 2, 4, 5)
+UNITS = (
+    (0, 256, 0, 2),
+    (256, 256, 0, 0),
+    (0, 256, 1, 0),
+    (256, 256, 1, None),
+    (512, 256, 0, 0),
+    (512, 256, 1, 0),
+    (768, 256, 0, None),
+    (768, 128, 1, None),
+    (896, 128, 1, None),
+)
 RUN = 4
 GROUP = P * PACK
 EARLY = GROUP + HALF
@@ -66,7 +75,7 @@ def tile_list_meltab_root_kernel(
         nc.sync.dma_start(offsets[:], offs)
         nc.sync.dma_start(raw_co[:].bitcast(I32), co_words[0].bitcast(I32))
         nc.sync.dma_start(raw_si[:].bitcast(I32), si_words[0].bitcast(I32))
-        nc.sync.dma_start(gain[:], gn.rearrange("(b p t) -> p b t", b=PASSES, t=PACK))
+        nc.scalar.dma_start(gain[:], gn.rearrange("(b p t) -> p b t", b=PASSES, t=PACK))
         nc.sync.dma_start(weight_rows[0:P:8, :].bitcast(I32), co_scales[0].bitcast(I32))
         nc.sync.dma_start(weight_rows[4:P:8, :].bitcast(I32), si_scales[0].bitcast(I32))
         nc.sync.dma_start(table_rows[0:P:8, :].bitcast(I32), tab_scales[0].bitcast(I32))
@@ -115,13 +124,13 @@ def tile_list_meltab_root_kernel(
         picked_planes = [plane[:, 0, GROUP : GROUP + HALF] for plane in planes]
         fb_plane = planes[1][:, :, GROUP + HALF :]
 
-        def first_stage(u, j0, width, b):
-            squares = work.tile([P, PACK, 2, width], F32, name="squares", bufs=3)
+        def first_stage(j0, width, b, vector_slice):
+            squares = work.tile([P, PACK, 2, width], F32, name="squares", bufs=4)
             per_bank = BANK // (2 * width)
             h, c0 = divmod(j0, HALF)
             scaled = None
             for t0 in range(0, PACK, per_bank):
-                bank = psum.tile([P, per_bank, 2, width], F32, name="bank", bufs=6)
+                bank = psum.tile([P, per_bank, 2, width], F32, name="bank", tag="bank", bufs=6)
                 for t in range(t0, t0 + per_bank):
                     s = b * PACK + t
                     for part, dealt in enumerate((dealt_co, dealt_si)):
@@ -137,15 +146,15 @@ def tile_list_meltab_root_kernel(
                 for t in range(t0, t0 + per_bank):
                     sums = bank[:, t - t0, :, :].rearrange("p a c -> p (a c)")
                     root = root_gain[:, b, t : t + 1]
-                    if t == 0 and u in VECTOR_UNITS:
+                    if t == vector_slice:
                         scaled = work.tile([P, 2 * width], F32, name="scaled", bufs=2)
                         nc.vector.tensor_scalar(scaled[:], sums, root, None, MULT)
                     else:
                         nc.scalar.activation(squares[:, t, :, :].rearrange("p a c -> p (a c)"), sums, SQUARE, scale=root)
             return squares, scaled
 
-        def square_on_vector(squares, scaled):
-            nc.vector.tensor_tensor(squares[:, 0, :, :].rearrange("p a c -> p (a c)"), scaled[:], scaled[:], MULT)
+        def square_on_vector(squares, scaled, t):
+            nc.vector.tensor_tensor(squares[:, t, :, :].rearrange("p a c -> p (a c)"), scaled[:], scaled[:], MULT)
 
         def power(squares, width):
             woven = work.tile([P, width * PACK], BF16, name="woven", align_bytes=64, bufs=3)
@@ -181,37 +190,45 @@ def tile_list_meltab_root_kernel(
             nc.scalar.activation(result[:].rearrange("p a c -> p (a c)"), sums[:].rearrange("p a c -> p (a c)"), SQRT)
             nc.sync.dma_start(out.rearrange("(a p) j -> p a j", p=P)[:, :, j0 : j0 + width], result[:])
 
-        units = []
-        j0 = 0
-        for width in CHUNKS:
-            for b in range(PASSES):
-                units.append((j0, width, b))
-            j0 = j0 + width
-
-        units[1], units[2] = units[2], units[1]
-
+        unread = psum.tile([P, BANK], F32, name="unread", tag="sums", bufs=2)
+        for warm in range(2):
+            nc.tensor.matmul_mx(
+                unread[:],
+                lhsT=dealt_co[:, 0 : 2 * P].bitcast(FP4X4),
+                lhsT_scale=weight_rows[:, 0:P],
+                rhs=table[:, 0:BANK].bitcast(FP8X4),
+                rhs_scale=table_rows[:, 0:BANK],
+                start=True,
+                stop=True,
+            )
         gather(0)
         place(nc.sync, late_planes, late_rows, 4)
+        chunks = [(j0, width) for j0, width, b, vector_slice in UNITS if b == PASSES - 1]
         made = {}
         powers = {}
         quantised = {}
         sums = {}
-        count = len(units)
+        count = len(UNITS)
         for u in range(count + 4):
             if u < count:
-                made[u] = first_stage(u, *units[u])
+                made[u] = first_stage(*UNITS[u])
             if 1 <= u <= count:
-                powers[u - 1] = power(made[u - 1][0], units[u - 1][1])
+                powers[u - 1] = power(made[u - 1][0], UNITS[u - 1][1])
             if u == 0:
                 gather(1)
-            if u in VECTOR_UNITS:
-                square_on_vector(*made[u])
+            if u < count and UNITS[u][3] is not None:
+                square_on_vector(*made[u], UNITS[u][3])
             if 2 <= u <= count + 1:
-                quantised[u - 2] = quantise(powers[u - 2], units[u - 2][1])
-            if 4 <= u and units[u - 4][2] == PASSES - 1:
-                finish(sums[units[u - 4][0]], units[u - 4][0], units[u - 4][1])
+                quantised[u - 2] = quantise(powers[u - 2], UNITS[u - 2][1])
+            if 4 <= u and UNITS[u - 4][2] == PASSES - 1:
+                finish(sums[UNITS[u - 4][0]], UNITS[u - 4][0], UNITS[u - 4][1])
             if 3 <= u <= count + 2:
-                j0, width, b = units[u - 3]
-                if b == 0:
-                    sums[j0] = psum.tile([P, N // P, width], F32, name="sums", bufs=2)
-                second_stage(sums[j0], width, b, *quantised[u - 3])
+                u0, u_width, b, vector_slice = UNITS[u - 3]
+                codes, plane = quantised[u - 3]
+                for j0, width in chunks:
+                    if u0 <= j0 < u0 + u_width:
+                        if b == 0 and j0 + width < J:
+                            sums[j0] = psum.tile([P, N // P, width], F32, name="sums", tag="sums", bufs=2)
+                        elif b == 0:
+                            sums[j0] = psum.tile([P, N // P, width], F32, name="last_sums", tag="bank", bufs=6)
+                        second_stage(sums[j0], width, b, codes[:, j0 - u0 : j0 - u0 + width], plane[:, j0 - u0 : j0 - u0 + width])

@@ -25,8 +25,8 @@ BANK = 512
 HALF = J // 2
 UNITS = (
     (0, 256, 0, 2),
-    (256, 256, 0, 0),
     (0, 256, 1, 0),
+    (256, 256, 0, 0),
     (256, 256, 1, None),
     (512, 256, 0, 0),
     (512, 256, 1, 0),
@@ -35,9 +35,6 @@ UNITS = (
     (896, 128, 1, None),
 )
 RUN = 4
-GROUP = P * PACK
-EARLY = GROUP + HALF
-LATE = GROUP + HALF + N
 
 
 def tile_list_meltab_root_kernel(
@@ -59,10 +56,10 @@ def tile_list_meltab_root_kernel(
         dealt_si = keep.tile([P, 2 * F], U8, name="dealt_si", align_bytes=64)
         picked_rows = keep.tile([P, J], U8, name="picked_rows", align_bytes=64)
         picked = keep.tile([P, J], U32, name="picked", align_bytes=64)
-        early_rows = keep.tile([P, EARLY], U8, name="early_rows", tag="rows_then_fb", align_bytes=64)
-        late_rows = keep.tile([P, LATE], U8, name="late_rows", align_bytes=64)
-        early_planes = keep.tile([P, 2 * EARLY], U8, name="early_planes", align_bytes=64)
-        late_planes = keep.tile([P, 2 * LATE], U8, name="late_planes", align_bytes=64)
+        early_rows = keep.tile([P, F + HALF], U8, name="early_rows", tag="rows_then_fb", align_bytes=64)
+        late_rows = keep.tile([P, HALF + PASSES * N], U8, name="late_rows", align_bytes=64)
+        early_planes = keep.tile([P, 2 * (F + HALF)], U8, name="early_planes", align_bytes=64)
+        late_planes = keep.tile([P, HALF + PASSES * N], U8, name="late_planes", align_bytes=64)
         gain = keep.tile([P, PASSES, PACK], F32, name="gain")
         root_gain = keep.tile([P, PASSES, PACK], F32, name="root_gain")
 
@@ -81,7 +78,7 @@ def tile_list_meltab_root_kernel(
         nc.sync.dma_start(table_rows[0:P:8, :].bitcast(I32), tab_scales[0].bitcast(I32))
         nc.sync.dma_start(table[:], tab_words[0].rearrange("p t i -> p (t i)").bitcast(I32))
         nc.sync.dma_start(
-            late_rows[0:P:4, GROUP + HALF :].bitcast(I32),
+            late_rows[0:P:8, HALF:].rearrange("q (b n) -> q b n", b=PASSES).bitcast(I32),
             fb_scales.rearrange("b q n -> q b n").bitcast(I32),
         )
 
@@ -109,20 +106,18 @@ def tile_list_meltab_root_kernel(
                     rows[32 * quad : 32 * quad + 32 : step, :].bitcast(I32),
                 )
 
-        deal(early_rows[:, 0:GROUP], weight_rows[:, 0:GROUP])
+        deal(early_rows[:, 0:F], weight_rows[:])
         gather_scales(0)
-        nc.vector.tensor_copy(early_rows[:, GROUP:].bitcast(I32), picked_rows[:, 0:HALF].bitcast(I32))
+        nc.vector.tensor_copy(early_rows[:, F:].bitcast(I32), picked_rows[:, 0:HALF].bitcast(I32))
         place(nc.sync, early_planes, early_rows, 4)
         deal(dealt_co[:].bitcast(U16), raw_co[:].bitcast(U16))
         deal(dealt_si[:].bitcast(U16), raw_si[:].bitcast(U16))
         fb_codes = keep.tile([P, PASSES, 2 * N], U8, name="fb_codes", tag="rows_then_fb", align_bytes=64)
-        nc.scalar.dma_start(fb_codes[:].bitcast(I32), fb_words.rearrange("b p w -> p b w").bitcast(I32))
-        deal(late_rows[:, 0:GROUP], weight_rows[:, GROUP:])
+        nc.sync.dma_start(fb_codes[:].bitcast(I32), fb_words.rearrange("b p w -> p b w").bitcast(I32))
         gather_scales(1)
-        nc.vector.tensor_copy(late_rows[:, GROUP : GROUP + HALF].bitcast(I32), picked_rows[:, HALF:].bitcast(I32))
-        planes = (early_planes[:].rearrange("p (a w) -> p a w", a=2), late_planes[:].rearrange("p (a w) -> p a w", a=2))
-        picked_planes = [plane[:, 0, GROUP : GROUP + HALF] for plane in planes]
-        fb_plane = planes[1][:, :, GROUP + HALF :]
+        nc.vector.tensor_copy(late_rows[:, 0:HALF].bitcast(I32), picked_rows[:, HALF:].bitcast(I32))
+        picked_planes = (early_planes[:, F : F + HALF], late_planes[:, 0:HALF])
+        fb_plane = late_planes[:, HALF:].rearrange("p (b n) -> p b n", b=PASSES)
 
         def first_stage(j0, width, b, vector_slice):
             squares = work.tile([P, PACK, 2, width], F32, name="squares", bufs=4)
@@ -137,7 +132,7 @@ def tile_list_meltab_root_kernel(
                         nc.tensor.matmul_mx(
                             bank[:, t - t0, part, :],
                             lhsT=dealt[:, 2 * P * s : 2 * P * (s + 1)].bitcast(FP4X4),
-                            lhsT_scale=planes[b][:, part, P * t : P * (t + 1)],
+                            lhsT_scale=early_planes[:, part * (F + HALF) + P * s : part * (F + HALF) + P * (s + 1)],
                             rhs=picked[:, j0 : j0 + width].bitcast(FP8X4),
                             rhs_scale=picked_planes[h][:, c0 : c0 + width],
                             start=True,
@@ -202,7 +197,7 @@ def tile_list_meltab_root_kernel(
                 stop=True,
             )
         gather(0)
-        place(nc.sync, late_planes, late_rows, 4)
+        place(nc.sync, late_planes, late_rows, 8)
         chunks = [(j0, width) for j0, width, b, vector_slice in UNITS if b == PASSES - 1]
         made = {}
         powers = {}

@@ -35,6 +35,7 @@ UNITS = (
     (896, 128, 1, None),
 )
 RUN = 4
+ROWS = 96
 
 
 def tile_list_meltab_root_kernel(
@@ -63,22 +64,22 @@ def tile_list_meltab_root_kernel(
         gain = keep.tile([P, PASSES, PACK], F32, name="gain")
         root_gain = keep.tile([P, PASSES, PACK], F32, name="root_gain")
 
-        nc.vector.memset(weight_rows[:].bitcast(I32), 0)
         nc.vector.memset(table_rows[:, 0 : T // 2].bitcast(I32), 0)
         nc.gpsimd.memset(table_rows[:, T // 2 :].bitcast(I32), 0)
+        nc.vector.memset(weight_rows[0:ROWS, :].bitcast(I32), 0)
         nc.vector.memset(early_planes[:].bitcast(I32), 0)
         nc.vector.memset(late_planes[:].bitcast(I32), 0)
 
         nc.sync.dma_start(offsets[:], offs)
+        nc.sync.dma_start(weight_rows[ROWS:P:2, :].bitcast(I32), co_scales[0].bitcast(I32))
+        nc.sync.dma_start(weight_rows[ROWS + 1 : P : 2, :].bitcast(I32), si_scales[0].bitcast(I32))
         nc.sync.dma_start(raw_co[:].bitcast(I32), co_words[0].bitcast(I32))
-        nc.sync.dma_start(raw_si[:].bitcast(I32), si_words[0].bitcast(I32))
         nc.scalar.dma_start(gain[:], gn.rearrange("(b p t) -> p b t", b=PASSES, t=PACK))
-        nc.sync.dma_start(weight_rows[0:P:8, :].bitcast(I32), co_scales[0].bitcast(I32))
-        nc.sync.dma_start(weight_rows[4:P:8, :].bitcast(I32), si_scales[0].bitcast(I32))
-        nc.sync.dma_start(table_rows[0:P:8, :].bitcast(I32), tab_scales[0].bitcast(I32))
+        nc.sync.dma_start(table_rows[ROWS:P:2, :].bitcast(I32), tab_scales[0].bitcast(I32))
+        nc.sync.dma_start(raw_si[:].bitcast(I32), si_words[0].bitcast(I32))
         nc.sync.dma_start(table[:], tab_words[0].rearrange("p t i -> p (t i)").bitcast(I32))
         nc.sync.dma_start(
-            late_rows[0:P:8, HALF:].rearrange("q (b n) -> q b n", b=PASSES).bitcast(I32),
+            late_rows[ROWS:P:2, HALF:].rearrange("q (b n) -> q b n", b=PASSES).bitcast(I32),
             fb_scales.rearrange("b q n -> q b n").bitcast(I32),
         )
 
@@ -103,14 +104,14 @@ def tile_list_meltab_root_kernel(
             for quad in range(4):
                 queue.dma_start(
                     planes[32 * quad : 32 * quad + 4, :].bitcast(I32),
-                    rows[32 * quad : 32 * quad + 32 : step, :].bitcast(I32),
+                    rows[ROWS + 8 * quad : ROWS + 8 * quad + 8 : step, :].bitcast(I32),
                 )
 
         deal(early_rows[:, 0:F], weight_rows[:])
+        deal(dealt_co[:].bitcast(U16), raw_co[:].bitcast(U16))
         gather_scales(0)
         nc.vector.tensor_copy(early_rows[:, F:].bitcast(I32), picked_rows[:, 0:HALF].bitcast(I32))
-        place(nc.sync, early_planes, early_rows, 4)
-        deal(dealt_co[:].bitcast(U16), raw_co[:].bitcast(U16))
+        place(nc.sync, early_planes, early_rows, 1)
         deal(dealt_si[:].bitcast(U16), raw_si[:].bitcast(U16))
         fb_codes = keep.tile([P, PASSES, 2 * N], U8, name="fb_codes", tag="rows_then_fb", align_bytes=64)
         nc.sync.dma_start(fb_codes[:].bitcast(I32), fb_words.rearrange("b p w -> p b w").bitcast(I32))
@@ -197,7 +198,7 @@ def tile_list_meltab_root_kernel(
                 stop=True,
             )
         gather(0)
-        place(nc.sync, late_planes, late_rows, 8)
+        place(nc.sync, late_planes, late_rows, 2)
         chunks = [(j0, width) for j0, width, b, vector_slice in UNITS if b == PASSES - 1]
         made = {}
         powers = {}

@@ -24,15 +24,15 @@ PASSES = F // (P * PACK)
 BANK = 512
 HALF = J // 2
 UNITS = (
-    (0, 256, 0, 2),
-    (0, 256, 1, 0),
-    (256, 256, 0, 0),
-    (256, 256, 1, None),
-    (512, 256, 0, 0),
-    (512, 256, 1, 0),
-    (768, 256, 0, None),
-    (768, 128, 1, None),
-    (896, 128, 1, None),
+    (0, 256, 0, "SSSS"),
+    (0, 256, 1, "GGPP"),
+    (256, 256, 0, "GPSS"),
+    (256, 256, 1, "SSSS"),
+    (512, 256, 0, "SSSS"),
+    (512, 256, 1, "SSSS"),
+    (768, 256, 0, "SSSS"),
+    (768, 128, 1, "SSSS"),
+    (896, 128, 1, "SSSS"),
 )
 RUN = 4
 ROWS = 96
@@ -77,7 +77,9 @@ def tile_list_meltab_root_kernel(
         nc.scalar.dma_start(gain[:], gn.rearrange("(b p t) -> p b t", b=PASSES, t=PACK))
         nc.sync.dma_start(table_rows[ROWS:P:2, :].bitcast(I32), tab_scales[0].bitcast(I32))
         nc.sync.dma_start(raw_si[:].bitcast(I32), si_words[0].bitcast(I32))
-        nc.sync.dma_start(table[:], tab_words[0].rearrange("p t i -> p (t i)").bitcast(I32))
+        words = tab_words[0].rearrange("p t i -> p (t i)").bitcast(I32)
+        nc.sync.dma_start(table[:, 0 : T // 2], words[:, 0 : T // 2])
+        nc.sync.dma_start(table[:, T // 2 :], words[:, T // 2 :])
         nc.sync.dma_start(
             late_rows[ROWS:P:2, HALF:].rearrange("q (b n) -> q b n", b=PASSES).bitcast(I32),
             fb_scales.rearrange("b q n -> q b n").bitcast(I32),
@@ -120,37 +122,53 @@ def tile_list_meltab_root_kernel(
         picked_planes = (early_planes[:, F : F + HALF], late_planes[:, 0:HALF])
         fb_plane = late_planes[:, HALF:].rearrange("p (b n) -> p b n", b=PASSES)
 
-        def first_stage(j0, width, b, vector_slice):
-            squares = work.tile([P, PACK, 2, width], F32, name="squares", bufs=4)
+        def fill(u, t0):
+            j0, width, b, plan = UNITS[u]
             per_bank = BANK // (2 * width)
             h, c0 = divmod(j0, HALF)
-            scaled = None
-            for t0 in range(0, PACK, per_bank):
-                bank = psum.tile([P, per_bank, 2, width], F32, name="bank", tag="bank", bufs=6)
-                for t in range(t0, t0 + per_bank):
-                    s = b * PACK + t
-                    for part, dealt in enumerate((dealt_co, dealt_si)):
-                        nc.tensor.matmul_mx(
-                            bank[:, t - t0, part, :],
-                            lhsT=dealt[:, 2 * P * s : 2 * P * (s + 1)].bitcast(FP4X4),
-                            lhsT_scale=early_planes[:, part * (F + HALF) + P * s : part * (F + HALF) + P * (s + 1)],
-                            rhs=picked[:, j0 : j0 + width].bitcast(FP8X4),
-                            rhs_scale=picked_planes[h][:, c0 : c0 + width],
-                            start=True,
-                            stop=True,
-                        )
-                for t in range(t0, t0 + per_bank):
-                    sums = bank[:, t - t0, :, :].rearrange("p a c -> p (a c)")
-                    root = root_gain[:, b, t : t + 1]
-                    if t == vector_slice:
-                        scaled = work.tile([P, 2 * width], F32, name="scaled", bufs=2)
-                        nc.vector.tensor_scalar(scaled[:], sums, root, None, MULT)
-                    else:
-                        nc.scalar.activation(squares[:, t, :, :].rearrange("p a c -> p (a c)"), sums, SQUARE, scale=root)
-            return squares, scaled
+            bank = psum.tile([P, per_bank, 2, width], F32, name="bank", tag="bank", bufs=6)
+            for t in range(t0, t0 + per_bank):
+                s = b * PACK + t
+                for part, dealt in enumerate((dealt_co, dealt_si)):
+                    nc.tensor.matmul_mx(
+                        bank[:, t - t0, part, :],
+                        lhsT=dealt[:, 2 * P * s : 2 * P * (s + 1)].bitcast(FP4X4),
+                        lhsT_scale=early_planes[:, part * (F + HALF) + P * s : part * (F + HALF) + P * (s + 1)],
+                        rhs=picked[:, j0 : j0 + width].bitcast(FP8X4),
+                        rhs_scale=picked_planes[h][:, c0 : c0 + width],
+                        start=True,
+                        stop=True,
+                    )
+            return [bank[:, i, :, :].rearrange("p a c -> p (a c)") for i in range(per_bank)]
 
-        def square_on_vector(squares, scaled, t):
-            nc.vector.tensor_tensor(squares[:, t, :, :].rearrange("p a c -> p (a c)"), scaled[:], scaled[:], MULT)
+        def row(squares, t):
+            return squares[:, t, :, :].rearrange("p a c -> p (a c)")
+
+        def read_bank(u, t, sums, squares):
+            j0, width, b, plan = UNITS[u]
+            root = root_gain[:, b, t : t + 1]
+            if plan[t] == "S":
+                nc.scalar.activation(row(squares, t), sums, SQUARE, scale=root)
+                return None
+            copied = work.tile([P, 2 * width], F32, name="copied", bufs=6)
+            if plan[t] == "P":
+                nc.vector.tensor_copy(copied[:], sums)
+            else:
+                nc.vector.tensor_scalar(copied[:], sums, root, None, MULT)
+            if plan[t] == "G":
+                nc.gpsimd.tensor_tensor(row(squares, t), copied[:], copied[:], MULT)
+                return None
+            return t, sums, copied
+
+        def square_on_vector(u, squares, t, sums, copied):
+            j0, width, b, plan = UNITS[u]
+            if plan[t] == "P":
+                nc.vector.scalar_tensor_tensor(row(squares, t), sums, gain[:, b, t : t + 1], copied[:], MULT, MULT)
+            else:
+                nc.vector.tensor_tensor(row(squares, t), copied[:], copied[:], MULT)
+
+        def squares_of(u):
+            return work.tile([P, PACK, 2, UNITS[u][1]], F32, name="squares", bufs=5)
 
         def power(squares, width):
             woven = work.tile([P, width * PACK], BF16, name="woven", align_bytes=64, bufs=3)
@@ -187,10 +205,10 @@ def tile_list_meltab_root_kernel(
             nc.sync.dma_start(out.rearrange("(a p) j -> p a j", p=P)[:, :, j0 : j0 + width], result[:])
 
         unread = psum.tile([P, BANK], F32, name="unread", tag="sums", bufs=2)
-        for warm in range(2):
+        for warm in range(4):
             nc.tensor.matmul_mx(
                 unread[:],
-                lhsT=dealt_co[:, 0 : 2 * P].bitcast(FP4X4),
+                lhsT=raw_co[:, 0 : 2 * P].bitcast(FP4X4),
                 lhsT_scale=weight_rows[:, 0:P],
                 rhs=table[:, 0:BANK].bitcast(FP8X4),
                 rhs_scale=table_rows[:, 0:BANK],
@@ -199,27 +217,40 @@ def tile_list_meltab_root_kernel(
             )
         gather(0)
         place(nc.sync, late_planes, late_rows, 2)
-        chunks = [(j0, width) for j0, width, b, vector_slice in UNITS if b == PASSES - 1]
-        made = {}
+        chunks = [(j0, width) for j0, width, b, plan in UNITS if b == PASSES - 1]
+        squares = {u: squares_of(u) for u in range(4)}
+        gather(1)
+        held = {}
+        for u, t in ((0, 0), (0, 1), (1, 0), (0, 2), (1, 1), (0, 3), (1, 2), (2, 2), (1, 3), (2, 3), (3, 0), (2, 0), (3, 1), (2, 1), (3, 2), (3, 3)):
+            if (u, t) == (2, 0):
+                square_on_vector(1, squares[1], *held[1, 2])
+            held[u, t] = read_bank(u, t, fill(u, t)[0], squares[u])
+            if (u, t) == (2, 1):
+                square_on_vector(1, squares[1], *held[1, 3])
+                square_on_vector(2, squares[2], *held[2, 1])
         powers = {}
         quantised = {}
         sums = {}
         count = len(UNITS)
-        for u in range(count + 4):
-            if u < count:
-                made[u] = first_stage(*UNITS[u])
-            if 1 <= u <= count:
-                powers[u - 1] = power(made[u - 1][0], UNITS[u - 1][1])
-            if u == 0:
-                gather(1)
-            if u < count and UNITS[u][3] is not None:
-                square_on_vector(*made[u], UNITS[u][3])
+        for u in range(1, count + 4):
+            left = []
+            if 4 <= u < count:
+                squares[u] = squares_of(u)
+                per_bank = BANK // (2 * UNITS[u][1])
+                for t0 in range(0, PACK, per_bank):
+                    for i, part_sums in enumerate(fill(u, t0)):
+                        left.append(read_bank(u, t0 + i, part_sums, squares[u]))
+            if u <= count:
+                powers[u - 1] = power(squares[u - 1], UNITS[u - 1][1])
+            for todo in left:
+                if todo is not None:
+                    square_on_vector(u, squares[u], *todo)
             if 2 <= u <= count + 1:
                 quantised[u - 2] = quantise(powers[u - 2], UNITS[u - 2][1])
             if 4 <= u and UNITS[u - 4][2] == PASSES - 1:
                 finish(sums[UNITS[u - 4][0]], UNITS[u - 4][0], UNITS[u - 4][1])
             if 3 <= u <= count + 2:
-                u0, u_width, b, vector_slice = UNITS[u - 3]
+                u0, u_width, b, plan = UNITS[u - 3]
                 codes, plane = quantised[u - 3]
                 for j0, width in chunks:
                     if u0 <= j0 < u0 + u_width:

@@ -77,9 +77,7 @@ def tile_list_meltab_root_kernel(
         nc.scalar.dma_start(gain[:], gn.rearrange("(b p t) -> p b t", b=PASSES, t=PACK))
         nc.sync.dma_start(table_rows[ROWS:P:2, :].bitcast(I32), tab_scales[0].bitcast(I32))
         nc.sync.dma_start(raw_si[:].bitcast(I32), si_words[0].bitcast(I32))
-        words = tab_words[0].rearrange("p t i -> p (t i)").bitcast(I32)
-        nc.sync.dma_start(table[:, 0 : T // 2], words[:, 0 : T // 2])
-        nc.sync.dma_start(table[:, T // 2 :], words[:, T // 2 :])
+        nc.sync.dma_start(table[:], tab_words[0].rearrange("p t i -> p (t i)").bitcast(I32))
         nc.sync.dma_start(
             late_rows[ROWS:P:2, HALF:].rearrange("q (b n) -> q b n", b=PASSES).bitcast(I32),
             fb_scales.rearrange("b q n -> q b n").bitcast(I32),
@@ -114,11 +112,11 @@ def tile_list_meltab_root_kernel(
         gather_scales(0)
         nc.vector.tensor_copy(early_rows[:, F:].bitcast(I32), picked_rows[:, 0:HALF].bitcast(I32))
         place(nc.sync, early_planes, early_rows, 1)
+        gather_scales(1)
+        nc.vector.tensor_copy(late_rows[:, 0:HALF].bitcast(I32), picked_rows[:, HALF:].bitcast(I32))
         deal(dealt_si[:].bitcast(U16), raw_si[:].bitcast(U16))
         fb_codes = keep.tile([P, PASSES, 2 * N], U8, name="fb_codes", tag="rows_then_fb", align_bytes=64)
         nc.sync.dma_start(fb_codes[:].bitcast(I32), fb_words.rearrange("b p w -> p b w").bitcast(I32))
-        gather_scales(1)
-        nc.vector.tensor_copy(late_rows[:, 0:HALF].bitcast(I32), picked_rows[:, HALF:].bitcast(I32))
         picked_planes = (early_planes[:, F : F + HALF], late_planes[:, 0:HALF])
         fb_plane = late_planes[:, HALF:].rearrange("p (b n) -> p b n", b=PASSES)
 
@@ -208,9 +206,9 @@ def tile_list_meltab_root_kernel(
         for warm in range(4):
             nc.tensor.matmul_mx(
                 unread[:],
-                lhsT=raw_co[:, 0 : 2 * P].bitcast(FP4X4),
+                lhsT=dealt_si[:, 0 : 2 * P].bitcast(FP4X4),
                 lhsT_scale=weight_rows[:, 0:P],
-                rhs=table[:, 0:BANK].bitcast(FP8X4),
+                rhs=table_rows[:, 0 : PACK * BANK].bitcast(FP8X4),
                 rhs_scale=table_rows[:, 0:BANK],
                 start=True,
                 stop=True,

@@ -101,7 +101,7 @@ def tile_list_meltab_root_kernel(
             nc.vector.tensor_copy(picked[:, h * HALF : (h + 1) * HALF], table[:].bitcast(U32).indirect(half_list(h)))
 
         def place(queue, planes, rows, step):
-            for quad in range(4):
+            for quad in (0, 2, 1, 3):
                 queue.dma_start(
                     planes[32 * quad : 32 * quad + 4, :].bitcast(I32),
                     rows[ROWS + 8 * quad : ROWS + 8 * quad + 8 : step, :].bitcast(I32),

@@ -20,20 +20,25 @@ SQRT = mybir.ActivationFunctionType.Sqrt
 
 P = 128
 PACK = 4
-PASSES = F // (P * PACK)
+F_PASS = P * PACK
+PASSES = F // F_PASS
 BANK = 512
 HALF = J // 2
+WIDE = 256
 UNITS = (
-    (0, 256, 0, "SSSS"),
-    (0, 256, 1, "GGPP"),
-    (256, 256, 0, "GPSS"),
-    (256, 256, 1, "SSSS"),
-    (512, 256, 0, "SSSS"),
-    (512, 256, 1, "SSSS"),
-    (768, 256, 0, "SSSS"),
-    (768, 128, 1, "SSSS"),
-    (896, 128, 1, "SSSS"),
+    (0, 256, 0),
+    (0, 256, 1),
+    (256, 256, 0),
+    (256, 256, 1),
+    (512, 256, 0),
+    (512, 256, 1),
+    (768, 256, 0),
+    (768, 128, 1),
+    (896, 128, 1),
 )
+GATHERS = ((0, 256), (256, 256), (512, 512))
+POOL_UNITS = 2
+VECTOR_BANKS = 6
 RUN = 4
 ROWS = 96
 
@@ -45,215 +50,211 @@ def tile_list_meltab_root_kernel(
     with ExitStack() as ctx:
         keep = ctx.enter_context(tc.tile_pool(name="keep", bufs=1))
         work = ctx.enter_context(tc.tile_pool(name="work", bufs=3))
+        turn = ctx.enter_context(tc.tile_pool(name="turn", bufs=1))
         psum = ctx.enter_context(tc.psum_pool(name="psum", bufs=1))
 
         offsets = keep.tile([P, J // 16], U16, name="offsets")
         table = keep.tile([P, T], I32, name="table", align_bytes=64)
-        table_rows = keep.tile([P, T], U8, name="table_rows", align_bytes=64)
-        weight_rows = keep.tile([P, F], U8, name="weight_rows", align_bytes=64)
-        raw_co = keep.tile([P, 2 * F], U8, name="raw_co", align_bytes=64)
+        table_rows = keep.tile([P, T], U8, name="table_rows", tag="rows_then_co", align_bytes=64)
+        rows = keep.tile([P, 2 * F + HALF], U8, name="rows", align_bytes=64)
+        weight_rows = rows[:, 0:F]
+        staged = rows[:, F:]
+        raw_co = keep.tile([P, 2 * F], U8, name="raw_co", tag="co_then_si", align_bytes=64)
         raw_si = keep.tile([P, 2 * F], U8, name="raw_si", align_bytes=64)
-        dealt_co = keep.tile([P, 2 * F], U8, name="dealt_co", align_bytes=64)
-        dealt_si = keep.tile([P, 2 * F], U8, name="dealt_si", align_bytes=64)
-        picked_rows = keep.tile([P, J], U8, name="picked_rows", align_bytes=64)
-        picked = keep.tile([P, J], U32, name="picked", align_bytes=64)
-        early_rows = keep.tile([P, F + HALF], U8, name="early_rows", tag="rows_then_fb", align_bytes=64)
-        late_rows = keep.tile([P, HALF + PASSES * N], U8, name="late_rows", align_bytes=64)
-        early_planes = keep.tile([P, 2 * (F + HALF)], U8, name="early_planes", align_bytes=64)
-        late_planes = keep.tile([P, HALF + PASSES * N], U8, name="late_planes", align_bytes=64)
+        dealt_co = keep.tile([P, F], U8, name="dealt_co", align_bytes=64)
+        picked_rows = [keep.tile([P, HALF], U8, name=f"picked_rows{h}", align_bytes=64) for h in range(2)]
+        picked = [keep.tile([P, width], U32, name=f"picked{g}", align_bytes=64) for g, (j0, width) in enumerate(GATHERS)]
+        first_planes = keep.tile([P, F + HALF], U8, name="first_planes", align_bytes=64)
+        second_planes = keep.tile([P, F], U8, name="second_planes", align_bytes=64)
+        late_plane = keep.tile([P, HALF], U8, name="late_plane", align_bytes=64)
+        fb_plane = keep.tile([P, PASSES, N], U8, name="fb_plane", align_bytes=64)
+        fb_codes = keep.tile([P, PASSES, 2 * N], U8, name="fb_codes", align_bytes=64)
         gain = keep.tile([P, PASSES, PACK], F32, name="gain")
         root_gain = keep.tile([P, PASSES, PACK], F32, name="root_gain")
 
         nc.vector.memset(table_rows[:, 0 : T // 2].bitcast(I32), 0)
         nc.gpsimd.memset(table_rows[:, T // 2 :].bitcast(I32), 0)
         nc.vector.memset(weight_rows[0:ROWS, :].bitcast(I32), 0)
-        nc.vector.memset(early_planes[:].bitcast(I32), 0)
-        nc.vector.memset(late_planes[:].bitcast(I32), 0)
+        nc.vector.memset(first_planes[:].bitcast(I32), 0)
+        nc.vector.memset(second_planes[:].bitcast(I32), 0)
+        nc.vector.memset(late_plane[:].bitcast(I32), 0)
+        nc.vector.memset(fb_plane[:].bitcast(I32), 0)
 
         nc.sync.dma_start(offsets[:], offs)
-        nc.sync.dma_start(weight_rows[ROWS:P:2, :].bitcast(I32), co_scales[0].bitcast(I32))
-        nc.sync.dma_start(weight_rows[ROWS + 1 : P : 2, :].bitcast(I32), si_scales[0].bitcast(I32))
+        for part, scales in enumerate((co_scales, si_scales)):
+            nc.sync.dma_start(
+                weight_rows[ROWS:P, part * F_PASS : (part + 1) * F_PASS].bitcast(I32),
+                scales[0].rearrange("q (b f) -> (q b) f", b=PASSES).bitcast(I32),
+            )
         nc.sync.dma_start(raw_co[:].bitcast(I32), co_words[0].bitcast(I32))
         nc.scalar.dma_start(gain[:], gn.rearrange("(b p t) -> p b t", b=PASSES, t=PACK))
         nc.sync.dma_start(table_rows[ROWS:P:2, :].bitcast(I32), tab_scales[0].bitcast(I32))
         nc.sync.dma_start(raw_si[:].bitcast(I32), si_words[0].bitcast(I32))
         nc.sync.dma_start(table[:], tab_words[0].rearrange("p t i -> p (t i)").bitcast(I32))
-        nc.sync.dma_start(
-            late_rows[ROWS:P:2, HALF:].rearrange("q (b n) -> q b n", b=PASSES).bitcast(I32),
-            fb_scales.rearrange("b q n -> q b n").bitcast(I32),
-        )
 
         nc.scalar.activation(root_gain[:], gain[:], SQRT)
 
-        def deal(dealt, raw):
+        def deal(target, raw):
             nc.vector.tensor_copy(
-                dealt.rearrange("p (g t q) -> p g t q", t=PACK, q=P),
+                target.rearrange("p (g t q) -> p g t q", t=PACK, q=P),
                 raw.rearrange("p (g q t) -> p g t q", t=PACK, q=P),
             )
 
-        def half_list(h):
-            return offsets[:, h * (HALF // 16) : (h + 1) * (HALF // 16)]
+        def entries(j0, width):
+            return offsets[:, j0 // 16 : (j0 + width) // 16]
 
-        def gather_scales(h):
-            nc.vector.tensor_copy(picked_rows[:, h * HALF : (h + 1) * HALF], table_rows[:].indirect(half_list(h)))
-
-        def gather(h):
-            nc.vector.tensor_copy(picked[:, h * HALF : (h + 1) * HALF], table[:].bitcast(U32).indirect(half_list(h)))
-
-        def place(queue, planes, rows, step):
+        def place(plane, rows, first):
             for quad in (0, 2, 1, 3):
-                queue.dma_start(
-                    planes[32 * quad : 32 * quad + 4, :].bitcast(I32),
-                    rows[ROWS + 8 * quad : ROWS + 8 * quad + 8 : step, :].bitcast(I32),
-                )
+                start = first + 8 * quad
+                nc.sync.dma_start(plane[32 * quad : 32 * quad + 4, :].bitcast(I32), rows[start : start + 7 : 2, :].bitcast(I32))
 
-        deal(early_rows[:, 0:F], weight_rows[:])
-        deal(dealt_co[:].bitcast(U16), raw_co[:].bitcast(U16))
-        gather_scales(0)
-        nc.vector.tensor_copy(early_rows[:, F:].bitcast(I32), picked_rows[:, 0:HALF].bitcast(I32))
-        place(nc.sync, early_planes, early_rows, 1)
-        gather_scales(1)
-        nc.vector.tensor_copy(late_rows[:, 0:HALF].bitcast(I32), picked_rows[:, HALF:].bitcast(I32))
+        deal(staged[:, 0:F], weight_rows)
+        deal(dealt_co[:].bitcast(U16), raw_co[:, 0:F].bitcast(U16))
+        nc.vector.tensor_copy(picked_rows[0][:], table_rows[:].indirect(entries(0, HALF)))
+        nc.vector.tensor_copy(staged[:, F:].bitcast(I32), picked_rows[0][:].bitcast(I32))
+        place(first_planes, staged, ROWS)
+        place(second_planes, staged[:, 0:F], ROWS + 1)
+        nc.vector.tensor_copy(picked_rows[1][:], table_rows[:].indirect(entries(HALF, HALF)))
+        late_co = keep.tile([P, F], U8, name="late_co", tag="rows_then_co", align_bytes=64)
+        deal(late_co[:].bitcast(U16), raw_co[:, F:].bitcast(U16))
+        dealt_si = keep.tile([P, 2 * F], U8, name="dealt_si", tag="co_then_si", align_bytes=64)
         deal(dealt_si[:].bitcast(U16), raw_si[:].bitcast(U16))
-        fb_codes = keep.tile([P, PASSES, 2 * N], U8, name="fb_codes", tag="rows_then_fb", align_bytes=64)
+        dealt = ((dealt_co[:], dealt_si[:, 0:F]), (late_co[:], dealt_si[:, F:]))
+        place(late_plane, picked_rows[1], ROWS)
+        for quad in range(4):
+            nc.sync.dma_start(
+                fb_plane[32 * quad : 32 * quad + 4, :, :].bitcast(I32),
+                fb_scales[:, 4 * quad : 4 * quad + 4, :].rearrange("b r n -> r b n").bitcast(I32),
+            )
         nc.sync.dma_start(fb_codes[:].bitcast(I32), fb_words.rearrange("b p w -> p b w").bitcast(I32))
-        picked_planes = (early_planes[:, F : F + HALF], late_planes[:, 0:HALF])
-        fb_plane = late_planes[:, HALF:].rearrange("p (b n) -> p b n", b=PASSES)
+        weight_planes = (first_planes, second_planes)
+        picked_planes = (first_planes[:, F:], late_plane[:])
+
+        unread = psum.tile([P, BANK], F32, name="unread", tag="sums", bufs=2)
+        for warm in range(4):
+            nc.tensor.matmul_mx(
+                unread[:],
+                lhsT=late_co[:, 0 : 2 * P].bitcast(FP4X4),
+                lhsT_scale=weight_rows[:, 0:P],
+                rhs=rows[:, 0 : PACK * BANK].bitcast(FP8X4),
+                rhs_scale=weight_rows[:, 0:BANK],
+                start=True,
+                stop=True,
+            )
+
+        for g, (j0, width) in enumerate(GATHERS):
+            nc.vector.tensor_copy(picked[g][:], table[:].bitcast(U32).indirect(entries(j0, width)))
 
         def fill(u, t0):
-            j0, width, b, plan = UNITS[u]
+            j0, width, b = UNITS[u]
             per_bank = BANK // (2 * width)
             h, c0 = divmod(j0, HALF)
+            g = max(i for i, (g0, g_width) in enumerate(GATHERS) if g0 <= j0)
+            g0 = j0 - GATHERS[g][0]
             bank = psum.tile([P, per_bank, 2, width], F32, name="bank", tag="bank", bufs=6)
             for t in range(t0, t0 + per_bank):
-                s = b * PACK + t
-                for part, dealt in enumerate((dealt_co, dealt_si)):
+                for part in range(2):
                     nc.tensor.matmul_mx(
                         bank[:, t - t0, part, :],
-                        lhsT=dealt[:, 2 * P * s : 2 * P * (s + 1)].bitcast(FP4X4),
-                        lhsT_scale=early_planes[:, part * (F + HALF) + P * s : part * (F + HALF) + P * (s + 1)],
-                        rhs=picked[:, j0 : j0 + width].bitcast(FP8X4),
+                        lhsT=dealt[b][part][:, 2 * P * t : 2 * P * (t + 1)].bitcast(FP4X4),
+                        lhsT_scale=weight_planes[b][:, part * F_PASS + P * t : part * F_PASS + P * (t + 1)],
+                        rhs=picked[g][:, g0 : g0 + width].bitcast(FP8X4),
                         rhs_scale=picked_planes[h][:, c0 : c0 + width],
                         start=True,
                         stop=True,
                     )
             return [bank[:, i, :, :].rearrange("p a c -> p (a c)") for i in range(per_bank)]
 
-        def row(squares, t):
-            return squares[:, t, :, :].rearrange("p a c -> p (a c)")
+        squares = [keep.tile([P, PACK, 2, width], F32, name=f"squares{u}") for u, (j0, width, b) in enumerate(UNITS)]
 
-        def read_bank(u, t, sums, squares):
-            j0, width, b, plan = UNITS[u]
-            root = root_gain[:, b, t : t + 1]
-            if plan[t] == "S":
-                nc.scalar.activation(row(squares, t), sums, SQUARE, scale=root)
-                return None
-            copied = work.tile([P, 2 * width], F32, name="copied", bufs=6)
-            if plan[t] == "P":
-                nc.vector.tensor_copy(copied[:], sums)
-            else:
-                nc.vector.tensor_scalar(copied[:], sums, root, None, MULT)
-            if plan[t] == "G":
-                nc.gpsimd.tensor_tensor(row(squares, t), copied[:], copied[:], MULT)
-                return None
-            return t, sums, copied
+        def row(u, t):
+            return squares[u][:, t, :, :].rearrange("p a c -> p (a c)")
 
-        def square_on_vector(u, squares, t, sums, copied):
-            j0, width, b, plan = UNITS[u]
-            if plan[t] == "P":
-                nc.vector.scalar_tensor_tensor(row(squares, t), sums, gain[:, b, t : t + 1], copied[:], MULT, MULT)
-            else:
-                nc.vector.tensor_tensor(row(squares, t), copied[:], copied[:], MULT)
+        def square_on_scalar(u, t0):
+            for i, sums in enumerate(fill(u, t0)):
+                nc.scalar.activation(row(u, t0 + i), sums, SQUARE, scale=root_gain[:, UNITS[u][2], t0 + i : t0 + i + 1])
 
-        def squares_of(u):
-            return work.tile([P, PACK, 2, UNITS[u][1]], F32, name="squares", bufs=5)
-
-        def power(squares, width):
-            woven = work.tile([P, width * PACK], BF16, name="woven", align_bytes=64, bufs=3)
-            nc.vector.tensor_tensor(
+        def power(engine, u, woven):
+            engine.tensor_tensor(
                 woven[:].rearrange("p (c i t) -> p c t i", i=RUN, t=PACK),
-                squares[:, :, 0, :].rearrange("p t (c i) -> p c t i", i=RUN),
-                squares[:, :, 1, :].rearrange("p t (c i) -> p c t i", i=RUN),
+                squares[u][:, :, 0, :].rearrange("p t (c i) -> p c t i", i=RUN),
+                squares[u][:, :, 1, :].rearrange("p t (c i) -> p c t i", i=RUN),
                 ADD,
             )
-            return woven
 
-        def quantise(woven, width):
-            codes = work.tile([P, width], U32, name="codes", align_bytes=64)
-            plane = work.tile([P, width], U8, name="plane", align_bytes=64)
-            nc.vector.quantize_mx(codes[:].bitcast(FP8X4), plane[:], woven[:])
-            return codes, plane
-
-        def second_stage(sums, width, b, codes, plane):
-            for a in range(N // P):
-                for c0 in range(0, width, P):
-                    nc.tensor.matmul_mx(
-                        sums[:, a, c0 : c0 + P],
-                        lhsT=fb_codes[:, b, 2 * P * a : 2 * P * (a + 1)].bitcast(FP4X4),
-                        lhsT_scale=fb_plane[:, b, P * a : P * (a + 1)],
-                        rhs=codes[:, c0 : c0 + P].bitcast(FP8X4),
-                        rhs_scale=plane[:, c0 : c0 + P],
-                        start=(b == 0 and a == 0 and c0 == 0),
-                        stop=(b == PASSES - 1 and a == N // P - 1 and c0 == width - P),
-                    )
-
-        def finish(sums, j0, width):
-            result = work.tile([P, N // P, width], F32, name="result")
-            nc.scalar.activation(result[:].rearrange("p a c -> p (a c)"), sums[:].rearrange("p a c -> p (a c)"), SQRT)
-            nc.sync.dma_start(out.rearrange("(a p) j -> p a j", p=P)[:, :, j0 : j0 + width], result[:])
-
-        unread = psum.tile([P, BANK], F32, name="unread", tag="sums", bufs=2)
-        for warm in range(4):
-            nc.tensor.matmul_mx(
-                unread[:],
-                lhsT=dealt_si[:, 0 : 2 * P].bitcast(FP4X4),
-                lhsT_scale=weight_rows[:, 0:P],
-                rhs=table_rows[:, 0 : PACK * BANK].bitcast(FP8X4),
-                rhs_scale=table_rows[:, 0:BANK],
-                start=True,
-                stop=True,
-            )
-        gather(0)
-        place(nc.sync, late_planes, late_rows, 2)
-        chunks = [(j0, width) for j0, width, b, plan in UNITS if b == PASSES - 1]
-        squares = {u: squares_of(u) for u in range(4)}
-        gather(1)
-        held = {}
-        for u, t in ((0, 0), (0, 1), (1, 0), (0, 2), (1, 1), (0, 3), (1, 2), (2, 2), (1, 3), (2, 3), (3, 0), (2, 0), (3, 1), (2, 1), (3, 2), (3, 3)):
-            if (u, t) == (2, 0):
-                square_on_vector(1, squares[1], *held[1, 2])
-            held[u, t] = read_bank(u, t, fill(u, t)[0], squares[u])
-            if (u, t) == (2, 1):
-                square_on_vector(1, squares[1], *held[1, 3])
-                square_on_vector(2, squares[2], *held[2, 1])
-        powers = {}
-        quantised = {}
         sums = {}
+        chunks = [(j0, width) for j0, width, b in UNITS if b == PASSES - 1]
+
+        def second_stage(u, woven, plane):
+            u0, u_width, b = UNITS[u]
+            codes = work.tile([P, u_width], U32, name="codes", align_bytes=64)
+            nc.vector.quantize_mx(codes[:].bitcast(FP8X4), plane[:], woven[:])
+            for j0, width in chunks:
+                if u0 <= j0 < u0 + u_width:
+                    if b == 0 and j0 + width < J:
+                        sums[j0] = psum.tile([P, N // P, width], F32, name="sums", tag="sums", bufs=2)
+                    elif b == 0:
+                        sums[j0] = psum.tile([P, N // P, width], F32, name="last_sums", tag="bank", bufs=6)
+                    for a in range(N // P):
+                        nc.tensor.matmul_mx(
+                            sums[j0][:, a, :],
+                            lhsT=fb_codes[:, b, 2 * P * a : 2 * P * (a + 1)].bitcast(FP4X4),
+                            lhsT_scale=fb_plane[:, b, P * a : P * (a + 1)],
+                            rhs=codes[:, j0 - u0 : j0 - u0 + width].bitcast(FP8X4),
+                            rhs_scale=plane[:, j0 - u0 : j0 - u0 + width],
+                            start=(b == 0 and a == 0),
+                            stop=(b == PASSES - 1 and a == N // P - 1),
+                        )
+
+        def finish(u):
+            j0, width, b = UNITS[u]
+            if b == PASSES - 1:
+                result = work.tile([P, N // P, width], F32, name="result")
+                nc.scalar.activation(result[:].rearrange("p a c -> p (a c)"), sums[j0][:].rearrange("p a c -> p (a c)"), SQRT)
+                nc.sync.dma_start(out.rearrange("(a p) j -> p a j", p=P)[:, :, j0 : j0 + width], result[:])
+
+        slices = [(u, t) for u in range(POOL_UNITS + 2) for t in range(PACK)]
+        first = POOL_UNITS * PACK
+        on_vector = slices[first : first + VECTOR_BANKS]
+        on_scalar = slices[:first] + slices[first + VECTOR_BANKS :] + [(POOL_UNITS + 2, t) for t in range(PACK)]
+        wovens = {}
+        waiting = None
+        taken = 0
+        for i, (u, t) in enumerate(on_scalar):
+            square_on_scalar(u, t)
+            if u < POOL_UNITS and t == PACK - 1:
+                wovens[u] = work.tile([P, WIDE * PACK], BF16, name="pool_woven", align_bytes=64, bufs=2)
+                power(nc.gpsimd, u, wovens[u])
+            if i >= 2 and i % 2 == 0 and taken < VECTOR_BANKS:
+                vu, vt = on_vector[taken]
+                bank = fill(vu, vt)[0]
+                if taken == VECTOR_BANKS - 1:
+                    copied = turn.tile([P, BANK], F32, name="last_copied", offset=0)
+                else:
+                    copied = work.tile([P, BANK], F32, name="copied")
+                nc.vector.tensor_copy(copied[:], bank)
+                if waiting is not None:
+                    nc.vector.scalar_tensor_tensor(*waiting, MULT, MULT)
+                waiting = (row(vu, vt), bank, gain[:, UNITS[vu][2], vt : vt + 1], copied[:])
+                taken = taken + 1
+        nc.vector.scalar_tensor_tensor(*waiting, MULT, MULT)
+
+        planes = {u: turn.tile([P, WIDE], U8, name=f"plane{u}", offset=WIDE * u, align_bytes=64) for u in range(POOL_UNITS)}
         count = len(UNITS)
-        for u in range(1, count + 4):
-            left = []
-            if 4 <= u < count:
-                squares[u] = squares_of(u)
-                per_bank = BANK // (2 * UNITS[u][1])
-                for t0 in range(0, PACK, per_bank):
-                    for i, part_sums in enumerate(fill(u, t0)):
-                        left.append(read_bank(u, t0 + i, part_sums, squares[u]))
-            if u <= count:
-                powers[u - 1] = power(squares[u - 1], UNITS[u - 1][1])
-            for todo in left:
-                if todo is not None:
-                    square_on_vector(u, squares[u], *todo)
-            if 2 <= u <= count + 1:
-                quantised[u - 2] = quantise(powers[u - 2], UNITS[u - 2][1])
-            if 4 <= u and UNITS[u - 4][2] == PASSES - 1:
-                finish(sums[UNITS[u - 4][0]], UNITS[u - 4][0], UNITS[u - 4][1])
-            if 3 <= u <= count + 2:
-                u0, u_width, b, plan = UNITS[u - 3]
-                codes, plane = quantised[u - 3]
-                for j0, width in chunks:
-                    if u0 <= j0 < u0 + u_width:
-                        if b == 0 and j0 + width < J:
-                            sums[j0] = psum.tile([P, N // P, width], F32, name="sums", tag="sums", bufs=2)
-                        elif b == 0:
-                            sums[j0] = psum.tile([P, N // P, width], F32, name="last_sums", tag="bank", bufs=6)
-                        second_stage(sums[j0], width, b, codes[:, j0 - u0 : j0 - u0 + width], plane[:, j0 - u0 : j0 - u0 + width])
+        for step in range(count + 2):
+            u = step + POOL_UNITS
+            if POOL_UNITS + 3 <= u + 1 < count:
+                for t0 in range(0, PACK, BANK // (2 * UNITS[u + 1][1])):
+                    square_on_scalar(u + 1, t0)
+            if step < POOL_UNITS:
+                second_stage(step, wovens[step], planes[step])
+            if u < count:
+                if u == POOL_UNITS:
+                    wovens[u] = turn.tile([P, WIDE * PACK], BF16, name="held_woven", offset=WIDE * POOL_UNITS, align_bytes=64)
+                else:
+                    wovens[u] = work.tile([P, UNITS[u][1] * PACK], BF16, name="woven", align_bytes=64)
+                power(nc.vector, u, wovens[u])
+            if POOL_UNITS <= u - 1 < count:
+                second_stage(u - 1, wovens[u - 1], work.tile([P, UNITS[u - 1][1]], U8, name="plane", align_bytes=64))
+            if 0 <= u - 2 < count:
+                finish(u - 2)

@@ -27,8 +27,8 @@ HALF = J // 2
 WIDE = 256
 UNITS = (
     (0, 256, 0),
-    (0, 256, 1),
     (256, 256, 0),
+    (0, 256, 1),
     (256, 256, 1),
     (512, 256, 0),
     (512, 256, 1),
@@ -40,6 +40,7 @@ GATHERS = ((0, 256), (256, 256), (512, 512))
 POOL_UNITS = 2
 VECTOR_BANKS = 6
 RUN = 4
+POOL_RUN = 2
 ROWS = 96
 
 
@@ -145,9 +146,8 @@ def tile_list_meltab_root_kernel(
         for g, (j0, width) in enumerate(GATHERS):
             nc.vector.tensor_copy(picked[g][:], table[:].bitcast(U32).indirect(entries(j0, width)))
 
-        def fill(u, t0):
-            j0, width, b = UNITS[u]
-            per_bank = BANK // (2 * width)
+        def fill(u, t0, per_bank, first, width):
+            j0, b = UNITS[u][0] + first, UNITS[u][2]
             h, c0 = divmod(j0, HALF)
             g = max(i for i, (g0, g_width) in enumerate(GATHERS) if g0 <= j0)
             g0 = j0 - GATHERS[g][0]
@@ -163,22 +163,20 @@ def tile_list_meltab_root_kernel(
                         start=True,
                         stop=True,
                     )
-            return [bank[:, i, :, :].rearrange("p a c -> p (a c)") for i in range(per_bank)]
+            return [bank[:, i, :, :] for i in range(per_bank)]
 
         squares = [keep.tile([P, PACK, 2, width], F32, name=f"squares{u}") for u, (j0, width, b) in enumerate(UNITS)]
 
-        def row(u, t):
-            return squares[u][:, t, :, :].rearrange("p a c -> p (a c)")
+        def square_on_scalar(u, t0, per_bank, first, width):
+            for i, bank in enumerate(fill(u, t0, per_bank, first, width)):
+                t = t0 + i
+                nc.scalar.activation(squares[u][:, t, :, first : first + width], bank, SQUARE, scale=root_gain[:, UNITS[u][2], t : t + 1])
 
-        def square_on_scalar(u, t0):
-            for i, sums in enumerate(fill(u, t0)):
-                nc.scalar.activation(row(u, t0 + i), sums, SQUARE, scale=root_gain[:, UNITS[u][2], t0 + i : t0 + i + 1])
-
-        def power(engine, u, woven):
+        def power(engine, run, u, woven, first, width):
             engine.tensor_tensor(
-                woven[:].rearrange("p (c i t) -> p c t i", i=RUN, t=PACK),
-                squares[u][:, :, 0, :].rearrange("p t (c i) -> p c t i", i=RUN),
-                squares[u][:, :, 1, :].rearrange("p t (c i) -> p c t i", i=RUN),
+                woven[:, PACK * first : PACK * (first + width)].rearrange("p (c i t) -> p c t i", i=run, t=PACK),
+                squares[u][:, :, 0, first : first + width].rearrange("p t (c i) -> p c t i", i=run),
+                squares[u][:, :, 1, first : first + width].rearrange("p t (c i) -> p c t i", i=run),
                 ADD,
             )
 
@@ -213,29 +211,29 @@ def tile_list_meltab_root_kernel(
                 nc.scalar.activation(result[:].rearrange("p a c -> p (a c)"), sums[j0][:].rearrange("p a c -> p (a c)"), SQRT)
                 nc.sync.dma_start(out.rearrange("(a p) j -> p a j", p=P)[:, :, j0 : j0 + width], result[:])
 
-        slices = [(u, t) for u in range(POOL_UNITS + 2) for t in range(PACK)]
-        first = POOL_UNITS * PACK
-        on_vector = slices[first : first + VECTOR_BANKS]
-        on_scalar = slices[:first] + slices[first + VECTOR_BANKS :] + [(POOL_UNITS + 2, t) for t in range(PACK)]
-        wovens = {}
+        on_vector = [(1, 2, WIDE), (1, 3, WIDE), (2, 0, WIDE), (2, 1, WIDE), (2, 2, WIDE), (2, 3, P)]
+        on_scalar = [(0, t0, 2, first, P) for first in (0, P) for t0 in (0, 2)] + [(1, t, 1, 0, WIDE) for t in (0, 1)]
+        on_scalar = on_scalar + [(2, 3, 1, P, P)] + [(u, t, 1, 0, WIDE) for u in (3, 4) for t in range(PACK)]
+        wovens = {u: keep.tile([P, WIDE * PACK], BF16, name=f"pool_woven{u}", align_bytes=64) for u in range(POOL_UNITS)}
         waiting = None
         taken = 0
-        for i, (u, t) in enumerate(on_scalar):
-            square_on_scalar(u, t)
-            if u < POOL_UNITS and t == PACK - 1:
-                wovens[u] = work.tile([P, WIDE * PACK], BF16, name="pool_woven", align_bytes=64, bufs=2)
-                power(nc.gpsimd, u, wovens[u])
+        for i, (u, t, per_bank, first, width) in enumerate(on_scalar):
+            square_on_scalar(u, t, per_bank, first, width)
+            if u == 0 and t == 2:
+                power(nc.gpsimd, POOL_RUN, u, wovens[u], first, width)
             if i >= 2 and i % 2 == 0 and taken < VECTOR_BANKS:
-                vu, vt = on_vector[taken]
-                bank = fill(vu, vt)[0]
+                vu, vt, columns = on_vector[taken]
+                bank = fill(vu, vt, 1, 0, columns)[0]
                 if taken == VECTOR_BANKS - 1:
-                    copied = turn.tile([P, BANK], F32, name="last_copied", offset=0)
+                    copied = turn.tile([P, 2, columns], F32, name="last_copied", offset=0)
                 else:
-                    copied = work.tile([P, BANK], F32, name="copied")
+                    copied = work.tile([P, 2, columns], F32, name="copied")
                 nc.vector.tensor_copy(copied[:], bank)
                 if waiting is not None:
                     nc.vector.scalar_tensor_tensor(*waiting, MULT, MULT)
-                waiting = (row(vu, vt), bank, gain[:, UNITS[vu][2], vt : vt + 1], copied[:])
+                if taken == 2:
+                    power(nc.gpsimd, POOL_RUN, 1, wovens[1], 0, WIDE)
+                waiting = (squares[vu][:, vt, :, 0:columns], bank, gain[:, UNITS[vu][2], vt : vt + 1], copied[:])
                 taken = taken + 1
         nc.vector.scalar_tensor_tensor(*waiting, MULT, MULT)
 
@@ -244,17 +242,18 @@ def tile_list_meltab_root_kernel(
         for step in range(count + 2):
             u = step + POOL_UNITS
             if POOL_UNITS + 3 <= u + 1 < count:
-                for t0 in range(0, PACK, BANK // (2 * UNITS[u + 1][1])):
-                    square_on_scalar(u + 1, t0)
+                per_bank = BANK // (2 * UNITS[u + 1][1])
+                for t0 in range(0, PACK, per_bank):
+                    square_on_scalar(u + 1, t0, per_bank, 0, UNITS[u + 1][1])
             if step < POOL_UNITS:
                 second_stage(step, wovens[step], planes[step])
             if u < count:
-                if u == POOL_UNITS:
+                if u == POOL_UNITS + 1:
                     wovens[u] = turn.tile([P, WIDE * PACK], BF16, name="held_woven", offset=WIDE * POOL_UNITS, align_bytes=64)
                 else:
                     wovens[u] = work.tile([P, UNITS[u][1] * PACK], BF16, name="woven", align_bytes=64)
-                power(nc.vector, u, wovens[u])
+                power(nc.vector, RUN, u, wovens[u], 0, UNITS[u][1])
             if POOL_UNITS <= u - 1 < count:
                 second_stage(u - 1, wovens[u - 1], work.tile([P, UNITS[u - 1][1]], U8, name="plane", align_bytes=64))
-            if 0 <= u - 2 < count:
-                finish(u - 2)
+            if 0 <= u - 3 < count:
+                finish(u - 3)

@@ -37,10 +37,8 @@ UNITS = (
     (896, 128, 1),
 )
 GATHERS = ((0, 256), (256, 256), (512, 512))
-POOL_UNITS = 2
-VECTOR_BANKS = 6
+POOL_UNITS = (0, 1, 3)
 RUN = 4
-POOL_RUN = 2
 ROWS = 96
 
 
@@ -172,11 +170,11 @@ def tile_list_meltab_root_kernel(
                 t = t0 + i
                 nc.scalar.activation(squares[u][:, t, :, first : first + width], bank, SQUARE, scale=root_gain[:, UNITS[u][2], t : t + 1])
 
-        def power(engine, run, u, woven, first, width):
+        def power(engine, u, woven, first, width):
             engine.tensor_tensor(
-                woven[:, PACK * first : PACK * (first + width)].rearrange("p (c i t) -> p c t i", i=run, t=PACK),
-                squares[u][:, :, 0, first : first + width].rearrange("p t (c i) -> p c t i", i=run),
-                squares[u][:, :, 1, first : first + width].rearrange("p t (c i) -> p c t i", i=run),
+                woven[:, PACK * first : PACK * (first + width)].rearrange("p (c i t) -> p c t i", i=RUN, t=PACK),
+                squares[u][:, :, 0, first : first + width].rearrange("p t (c i) -> p c t i", i=RUN),
+                squares[u][:, :, 1, first : first + width].rearrange("p t (c i) -> p c t i", i=RUN),
                 ADD,
             )
 
@@ -211,49 +209,60 @@ def tile_list_meltab_root_kernel(
                 nc.scalar.activation(result[:].rearrange("p a c -> p (a c)"), sums[j0][:].rearrange("p a c -> p (a c)"), SQRT)
                 nc.sync.dma_start(out.rearrange("(a p) j -> p a j", p=P)[:, :, j0 : j0 + width], result[:])
 
-        on_vector = [(1, 2, WIDE), (1, 3, WIDE), (2, 0, WIDE), (2, 1, WIDE), (2, 2, WIDE), (2, 3, P)]
+        groups = (((1, 2, WIDE), (1, 3, WIDE)), ((2, 0, WIDE), (2, 1, WIDE)), ((4, 0, P), (2, 2, WIDE), (2, 3, WIDE)))
         on_scalar = [(0, t0, 2, first, P) for first in (0, P) for t0 in (0, 2)] + [(1, t, 1, 0, WIDE) for t in (0, 1)]
-        on_scalar = on_scalar + [(2, 3, 1, P, P)] + [(u, t, 1, 0, WIDE) for u in (3, 4) for t in range(PACK)]
-        wovens = {u: keep.tile([P, WIDE * PACK], BF16, name=f"pool_woven{u}", align_bytes=64) for u in range(POOL_UNITS)}
-        waiting = None
-        taken = 0
+        on_scalar = on_scalar + [(3, t, 1, 0, WIDE) for t in range(PACK)] + [(4, 0, 1, P, P)] + [(4, t, 1, 0, WIDE) for t in (1, 2, 3)]
+        wovens = {u: keep.tile([P, WIDE * PACK], BF16, name=f"pool_woven{u}", align_bytes=64) for u in POOL_UNITS}
         for i, (u, t, per_bank, first, width) in enumerate(on_scalar):
             square_on_scalar(u, t, per_bank, first, width)
             if u == 0 and t == 2:
-                power(nc.gpsimd, POOL_RUN, u, wovens[u], first, width)
-            if i >= 2 and i % 2 == 0 and taken < VECTOR_BANKS:
-                vu, vt, columns = on_vector[taken]
-                bank = fill(vu, vt, 1, 0, columns)[0]
-                if taken == VECTOR_BANKS - 1:
-                    copied = turn.tile([P, 2, columns], F32, name="last_copied", offset=0)
-                else:
-                    copied = work.tile([P, 2, columns], F32, name="copied")
-                nc.vector.tensor_copy(copied[:], bank)
-                if waiting is not None:
-                    nc.vector.scalar_tensor_tensor(*waiting, MULT, MULT)
-                if taken == 2:
-                    power(nc.gpsimd, POOL_RUN, 1, wovens[1], 0, WIDE)
-                waiting = (squares[vu][:, vt, :, 0:columns], bank, gain[:, UNITS[vu][2], vt : vt + 1], copied[:])
-                taken = taken + 1
-        nc.vector.scalar_tensor_tensor(*waiting, MULT, MULT)
+                power(nc.gpsimd, u, wovens[u], first, width)
+            if (u, t) == (1, 1) or (u, t) == (3, 3):
+                power(nc.gpsimd, u, wovens[u], 0, WIDE)
+            if i % 4 == 2 and i // 4 < len(groups):
+                pending = []
+                for vu, vt, columns in groups[i // 4]:
+                    bank = fill(vu, vt, 1, 0, columns)[0]
+                    if (vu, vt) == (2, 3):
+                        copied = turn.tile([P, 2, columns], F32, name="last_copied", offset=0)
+                    else:
+                        copied = work.tile([P, 2, columns], F32, name="copied")
+                    nc.vector.tensor_copy(copied[:], bank)
+                    pending.append((squares[vu][:, vt, :, 0:columns], bank, gain[:, UNITS[vu][2], vt : vt + 1], copied[:]))
+                for operands in pending:
+                    nc.vector.scalar_tensor_tensor(*operands, MULT, MULT)
 
-        planes = {u: turn.tile([P, WIDE], U8, name=f"plane{u}", offset=WIDE * u, align_bytes=64) for u in range(POOL_UNITS)}
+        def add_on_vector(u):
+            wovens[u] = work.tile([P, UNITS[u][1] * PACK], BF16, name="woven", align_bytes=64)
+            power(nc.vector, u, wovens[u], 0, UNITS[u][1])
+
+        def squares_of(u):
+            per_bank = BANK // (2 * UNITS[u][1])
+            for t0 in range(0, PACK, per_bank):
+                square_on_scalar(u, t0, per_bank, 0, UNITS[u][1])
+
+        def plane_of(u):
+            if u < 2:
+                return turn.tile([P, WIDE], U8, name=f"plane{u}", offset=WIDE * u, align_bytes=64)
+            return work.tile([P, UNITS[u][1]], U8, name="plane", align_bytes=64)
+
+        squares_of(5)
+        second_stage(0, wovens[0], plane_of(0))
+        add_on_vector(2)
+        second_stage(1, wovens[1], plane_of(1))
+        second_stage(3, wovens[3], plane_of(3))
+        second_stage(2, wovens[2], plane_of(2))
         count = len(UNITS)
-        for step in range(count + 2):
-            u = step + POOL_UNITS
-            if POOL_UNITS + 3 <= u + 1 < count:
-                per_bank = BANK // (2 * UNITS[u + 1][1])
-                for t0 in range(0, PACK, per_bank):
-                    square_on_scalar(u + 1, t0, per_bank, 0, UNITS[u + 1][1])
-            if step < POOL_UNITS:
-                second_stage(step, wovens[step], planes[step])
+        for u in range(4, count + 3):
+            if u + 2 < count:
+                squares_of(u + 2)
             if u < count:
-                if u == POOL_UNITS + 1:
-                    wovens[u] = turn.tile([P, WIDE * PACK], BF16, name="held_woven", offset=WIDE * POOL_UNITS, align_bytes=64)
-                else:
-                    wovens[u] = work.tile([P, UNITS[u][1] * PACK], BF16, name="woven", align_bytes=64)
-                power(nc.vector, RUN, u, wovens[u], 0, UNITS[u][1])
-            if POOL_UNITS <= u - 1 < count:
-                second_stage(u - 1, wovens[u - 1], work.tile([P, UNITS[u - 1][1]], U8, name="plane", align_bytes=64))
-            if 0 <= u - 3 < count:
-                finish(u - 3)
+                add_on_vector(u)
+            if 4 <= u - 1 < count:
+                second_stage(u - 1, wovens[u - 1], plane_of(u - 1))
+            if u == 4:
+                finish(3)
+            elif u == 5:
+                finish(2)
+            elif u - 2 < count:
+                finish(u - 2)

@@ -37,7 +37,7 @@ UNITS = (
     (896, 128, 1),
 )
 GATHERS = ((0, 256), (256, 256), (512, 512))
-POOL_UNITS = (0, 1, 3)
+POOL_PART = 128
 RUN = 4
 ROWS = 96
 
@@ -129,7 +129,7 @@ def tile_list_meltab_root_kernel(
         weight_planes = (first_planes, second_planes)
         picked_planes = (first_planes[:, F:], late_plane[:])
 
-        unread = psum.tile([P, BANK], F32, name="unread", tag="sums", bufs=2)
+        unread = psum.tile([P, BANK], F32, name="unread", tag="bank7")
         for warm in range(4):
             nc.tensor.matmul_mx(
                 unread[:],
@@ -144,12 +144,12 @@ def tile_list_meltab_root_kernel(
         for g, (j0, width) in enumerate(GATHERS):
             nc.vector.tensor_copy(picked[g][:], table[:].bitcast(U32).indirect(entries(j0, width)))
 
-        def fill(u, t0, per_bank, first, width):
+        def fill(place_in, u, t0, per_bank, first, width):
             j0, b = UNITS[u][0] + first, UNITS[u][2]
             h, c0 = divmod(j0, HALF)
             g = max(i for i, (g0, g_width) in enumerate(GATHERS) if g0 <= j0)
             g0 = j0 - GATHERS[g][0]
-            bank = psum.tile([P, per_bank, 2, width], F32, name="bank", tag="bank", bufs=6)
+            bank = psum.tile([P, per_bank, 2, width], F32, name="bank", tag=f"bank{place_in}")
             for t in range(t0, t0 + per_bank):
                 for part in range(2):
                     nc.tensor.matmul_mx(
@@ -163,16 +163,20 @@ def tile_list_meltab_root_kernel(
                     )
             return [bank[:, i, :, :] for i in range(per_bank)]
 
-        squares = [keep.tile([P, PACK, 2, width], F32, name=f"squares{u}") for u, (j0, width, b) in enumerate(UNITS)]
+        squares = [keep.tile([P, PACK, 2, width], F32, name=f"squares{u}", align_bytes=64) for u, (j0, width, b) in enumerate(UNITS)]
+
+        scalar_banks = [i % 4 for i in range(15)] + [6, 7] + [i % 4 for i in range(15, 25)]
+        vector_banks = [4, 5, 6, 7, 4, 5]
+        sum_banks = [6, 7, 4, 5, 6]
 
         def square_on_scalar(u, t0, per_bank, first, width):
-            for i, bank in enumerate(fill(u, t0, per_bank, first, width)):
+            for i, bank in enumerate(fill(scalar_banks.pop(0), u, t0, per_bank, first, width)):
                 t = t0 + i
                 nc.scalar.activation(squares[u][:, t, :, first : first + width], bank, SQUARE, scale=root_gain[:, UNITS[u][2], t : t + 1])
 
         def power(engine, u, woven, first, width):
             engine.tensor_tensor(
-                woven[:, PACK * first : PACK * (first + width)].rearrange("p (c i t) -> p c t i", i=RUN, t=PACK),
+                woven.rearrange("p (c i t) -> p c t i", i=RUN, t=PACK),
                 squares[u][:, :, 0, first : first + width].rearrange("p t (c i) -> p c t i", i=RUN),
                 squares[u][:, :, 1, first : first + width].rearrange("p t (c i) -> p c t i", i=RUN),
                 ADD,
@@ -181,48 +185,50 @@ def tile_list_meltab_root_kernel(
         sums = {}
         chunks = [(j0, width) for j0, width, b in UNITS if b == PASSES - 1]
 
-        def second_stage(u, woven, plane):
-            u0, u_width, b = UNITS[u]
-            codes = work.tile([P, u_width], U32, name="codes", align_bytes=64)
+        def second_stage(u, woven, plane, first=0, columns=None):
+            b = UNITS[u][2]
+            u0, u_width = UNITS[u][0] + first, columns or UNITS[u][1]
+            codes = work.tile([P, u_width], U32, name="codes", align_bytes=64, bufs=5)
             nc.vector.quantize_mx(codes[:].bitcast(FP8X4), plane[:], woven[:])
             for j0, width in chunks:
-                if u0 <= j0 < u0 + u_width:
-                    if b == 0 and j0 + width < J:
-                        sums[j0] = psum.tile([P, N // P, width], F32, name="sums", tag="sums", bufs=2)
-                    elif b == 0:
-                        sums[j0] = psum.tile([P, N // P, width], F32, name="last_sums", tag="bank", bufs=6)
+                lo, hi = max(j0, u0), min(j0 + width, u0 + u_width)
+                if lo < hi:
+                    if b == 0:
+                        sums[j0] = psum.tile([P, N // P, width], F32, name="sums", tag=f"bank{sum_banks.pop(0)}")
                     for a in range(N // P):
                         nc.tensor.matmul_mx(
-                            sums[j0][:, a, :],
+                            sums[j0][:, a, lo - j0 : hi - j0],
                             lhsT=fb_codes[:, b, 2 * P * a : 2 * P * (a + 1)].bitcast(FP4X4),
                             lhsT_scale=fb_plane[:, b, P * a : P * (a + 1)],
-                            rhs=codes[:, j0 - u0 : j0 - u0 + width].bitcast(FP8X4),
-                            rhs_scale=plane[:, j0 - u0 : j0 - u0 + width],
+                            rhs=codes[:, lo - u0 : hi - u0].bitcast(FP8X4),
+                            rhs_scale=plane[:, lo - u0 : hi - u0],
                             start=(b == 0 and a == 0),
-                            stop=(b == PASSES - 1 and a == N // P - 1),
+                            stop=(b == PASSES - 1 and a == N // P - 1 and hi == j0 + width),
                         )
 
         def finish(u):
             j0, width, b = UNITS[u]
             if b == PASSES - 1:
-                result = work.tile([P, N // P, width], F32, name="result")
+                result = work.tile([P, N // P, width], F32, name="result", bufs=5)
                 nc.scalar.activation(result[:].rearrange("p a c -> p (a c)"), sums[j0][:].rearrange("p a c -> p (a c)"), SQRT)
                 nc.sync.dma_start(out.rearrange("(a p) j -> p a j", p=P)[:, :, j0 : j0 + width], result[:])
 
-        groups = (((1, 2, WIDE), (1, 3, WIDE)), ((2, 0, WIDE), (2, 1, WIDE)), ((4, 0, P), (2, 2, WIDE), (2, 3, WIDE)))
-        on_scalar = [(0, t0, 2, first, P) for first in (0, P) for t0 in (0, 2)] + [(1, t, 1, 0, WIDE) for t in (0, 1)]
-        on_scalar = on_scalar + [(3, t, 1, 0, WIDE) for t in range(PACK)] + [(4, 0, 1, P, P)] + [(4, t, 1, 0, WIDE) for t in (1, 2, 3)]
-        wovens = {u: keep.tile([P, WIDE * PACK], BF16, name=f"pool_woven{u}", align_bytes=64) for u in POOL_UNITS}
+        groups = (((1, 2, WIDE), (1, 3, WIDE)), ((2, 0, WIDE), (2, 1, WIDE)), ((2, 2, WIDE), (2, 3, WIDE)))
+        on_scalar = [(0, 0, 1, 0, P), (0, 1, 1, 0, P), (0, 2, 2, 0, P), (0, 0, 2, P, P), (0, 2, 2, P, P)] + [(1, t, 1, 0, WIDE) for t in (0, 1)]
+        on_scalar = on_scalar + [(u, t, 1, 0, WIDE) for u in (3, 4) for t in range(PACK)]
+        wovens = {u: keep.tile([P, PACK * columns], BF16, name=f"pool_woven{u}", align_bytes=64) for u, columns in ((0, WIDE), (1, WIDE), (3, POOL_PART))}
         for i, (u, t, per_bank, first, width) in enumerate(on_scalar):
             square_on_scalar(u, t, per_bank, first, width)
             if u == 0 and t == 2:
-                power(nc.gpsimd, u, wovens[u], first, width)
-            if (u, t) == (1, 1) or (u, t) == (3, 3):
-                power(nc.gpsimd, u, wovens[u], 0, WIDE)
-            if i % 4 == 2 and i // 4 < len(groups):
+                power(nc.gpsimd, u, wovens[u][:, PACK * first : PACK * (first + width)], first, width)
+            if (u, t) == (1, 1):
+                power(nc.gpsimd, u, wovens[u][:], 0, WIDE)
+            if (u, t) == (3, 3):
+                power(nc.gpsimd, u, wovens[u][:], 0, POOL_PART)
+            if i % 4 == 3 and i // 4 < len(groups):
                 pending = []
                 for vu, vt, columns in groups[i // 4]:
-                    bank = fill(vu, vt, 1, 0, columns)[0]
+                    bank = fill(vector_banks.pop(0), vu, vt, 1, 0, columns)[0]
                     if (vu, vt) == (2, 3):
                         copied = turn.tile([P, 2, columns], F32, name="last_copied", offset=0)
                     else:
@@ -234,7 +240,7 @@ def tile_list_meltab_root_kernel(
 
         def add_on_vector(u):
             wovens[u] = work.tile([P, UNITS[u][1] * PACK], BF16, name="woven", align_bytes=64)
-            power(nc.vector, u, wovens[u], 0, UNITS[u][1])
+            power(nc.vector, u, wovens[u][:], 0, UNITS[u][1])
 
         def squares_of(u):
             per_bank = BANK // (2 * UNITS[u][1])
@@ -244,14 +250,17 @@ def tile_list_meltab_root_kernel(
         def plane_of(u):
             if u < 2:
                 return turn.tile([P, WIDE], U8, name=f"plane{u}", offset=WIDE * u, align_bytes=64)
-            return work.tile([P, UNITS[u][1]], U8, name="plane", align_bytes=64)
+            return work.tile([P, UNITS[u][1]], U8, name="plane", align_bytes=64, bufs=5)
 
         squares_of(5)
         second_stage(0, wovens[0], plane_of(0))
         add_on_vector(2)
         second_stage(1, wovens[1], plane_of(1))
-        second_stage(3, wovens[3], plane_of(3))
+        rest = turn.tile([P, PACK * (WIDE - POOL_PART)], BF16, name="rest", offset=2 * WIDE, align_bytes=64)
+        power(nc.vector, 3, rest[:], POOL_PART, WIDE - POOL_PART)
         second_stage(2, wovens[2], plane_of(2))
+        second_stage(3, wovens[3], keep.tile([P, POOL_PART], U8, name="pool_plane", tag="squares3", align_bytes=64), 0, POOL_PART)
+        second_stage(3, rest, plane_of(7), POOL_PART, WIDE - POOL_PART)
         count = len(UNITS)
         for u in range(4, count + 3):
             if u + 2 < count:
@@ -260,9 +269,7 @@ def tile_list_meltab_root_kernel(
                 add_on_vector(u)
             if 4 <= u - 1 < count:
                 second_stage(u - 1, wovens[u - 1], plane_of(u - 1))
-            if u == 4:
+            if u == 6:
                 finish(3)
-            elif u == 5:
-                finish(2)
-            elif u - 2 < count:
+            elif u != 5 and u - 2 < count:
                 finish(u - 2)

@@ -26,20 +26,19 @@ BANK = 512
 HALF = J // 2
 WIDE = 256
 UNITS = (
-    (0, 256, 0),
-    (256, 256, 0),
-    (0, 256, 1),
-    (256, 256, 1),
+    (0, 512, 0),
+    (0, 512, 1),
     (512, 256, 0),
     (512, 256, 1),
     (768, 256, 0),
     (768, 128, 1),
     (896, 128, 1),
 )
+CHUNKS = ((0, 512, (0,)), (0, 512, (1,)), (512, 256, (0, 1)), (768, 128, (0, 1)), (896, 128, (0, 1)))
 GATHERS = ((0, 256), (256, 256), (512, 512))
 POOL_PART = 128
 RUN = 4
-ROWS = 96
+ROWS = 32
 
 
 def tile_list_meltab_root_kernel(
@@ -49,19 +48,18 @@ def tile_list_meltab_root_kernel(
     with ExitStack() as ctx:
         keep = ctx.enter_context(tc.tile_pool(name="keep", bufs=1))
         work = ctx.enter_context(tc.tile_pool(name="work", bufs=3))
-        turn = ctx.enter_context(tc.tile_pool(name="turn", bufs=1))
         psum = ctx.enter_context(tc.psum_pool(name="psum", bufs=1))
 
         offsets = keep.tile([P, J // 16], U16, name="offsets")
         table = keep.tile([P, T], I32, name="table", align_bytes=64)
-        table_rows = keep.tile([P, T], U8, name="table_rows", tag="rows_then_co", align_bytes=64)
-        rows = keep.tile([P, 2 * F + HALF], U8, name="rows", align_bytes=64)
-        weight_rows = rows[:, 0:F]
-        staged = rows[:, F:]
-        raw_co = keep.tile([P, 2 * F], U8, name="raw_co", tag="co_then_si", align_bytes=64)
+        table_rows = keep.tile([P, T], U8, name="table_rows", align_bytes=64)
+        weight_rows = keep.tile([P, F], U8, name="weight_rows", tag="rows_then_picked", align_bytes=64)
+        staged = keep.tile([P, F + HALF], U8, name="staged", align_bytes=64)
+        raw_co = keep.tile([P, 2 * F], U8, name="raw_co", align_bytes=64)
         raw_si = keep.tile([P, 2 * F], U8, name="raw_si", align_bytes=64)
-        dealt_co = keep.tile([P, F], U8, name="dealt_co", align_bytes=64)
-        picked_rows = [keep.tile([P, HALF], U8, name=f"picked_rows{h}", align_bytes=64) for h in range(2)]
+        dealt_co = keep.tile([P, 2 * F], U8, name="dealt_co", align_bytes=64)
+        early_rows = keep.tile([P, HALF], U8, name="early_rows", align_bytes=64)
+        dealt_si = keep.tile([P, 2 * F], U8, name="dealt_si", align_bytes=64)
         picked = [keep.tile([P, width], U32, name=f"picked{g}", align_bytes=64) for g, (j0, width) in enumerate(GATHERS)]
         first_planes = keep.tile([P, F + HALF], U8, name="first_planes", align_bytes=64)
         second_planes = keep.tile([P, F], U8, name="second_planes", align_bytes=64)
@@ -71,24 +69,24 @@ def tile_list_meltab_root_kernel(
         gain = keep.tile([P, PASSES, PACK], F32, name="gain")
         root_gain = keep.tile([P, PASSES, PACK], F32, name="root_gain")
 
+        nc.vector.memset(weight_rows[:].bitcast(I32), 0)
         nc.vector.memset(table_rows[:, 0 : T // 2].bitcast(I32), 0)
         nc.gpsimd.memset(table_rows[:, T // 2 :].bitcast(I32), 0)
-        nc.vector.memset(weight_rows[0:ROWS, :].bitcast(I32), 0)
         nc.vector.memset(first_planes[:].bitcast(I32), 0)
         nc.vector.memset(second_planes[:].bitcast(I32), 0)
         nc.vector.memset(late_plane[:].bitcast(I32), 0)
         nc.vector.memset(fb_plane[:].bitcast(I32), 0)
 
+        nc.sync.dma_start(raw_co[:].bitcast(I32), co_words[0].bitcast(I32))
         nc.sync.dma_start(offsets[:], offs)
+        nc.sync.dma_start(raw_si[:].bitcast(I32), si_words[0].bitcast(I32))
+        nc.scalar.dma_start(gain[:], gn.rearrange("(b p t) -> p b t", b=PASSES, t=PACK))
+        nc.sync.dma_start(table_rows[ROWS : ROWS + 61 : 4, :].bitcast(I32), tab_scales[0].bitcast(I32))
         for part, scales in enumerate((co_scales, si_scales)):
             nc.sync.dma_start(
-                weight_rows[ROWS:P, part * F_PASS : (part + 1) * F_PASS].bitcast(I32),
+                weight_rows[ROWS : ROWS + 63 : 2, part * F_PASS : (part + 1) * F_PASS].bitcast(I32),
                 scales[0].rearrange("q (b f) -> (q b) f", b=PASSES).bitcast(I32),
             )
-        nc.sync.dma_start(raw_co[:].bitcast(I32), co_words[0].bitcast(I32))
-        nc.scalar.dma_start(gain[:], gn.rearrange("(b p t) -> p b t", b=PASSES, t=PACK))
-        nc.sync.dma_start(table_rows[ROWS:P:2, :].bitcast(I32), tab_scales[0].bitcast(I32))
-        nc.sync.dma_start(raw_si[:].bitcast(I32), si_words[0].bitcast(I32))
         nc.sync.dma_start(table[:], tab_words[0].rearrange("p t i -> p (t i)").bitcast(I32))
 
         nc.scalar.activation(root_gain[:], gain[:], SQRT)
@@ -104,22 +102,20 @@ def tile_list_meltab_root_kernel(
 
         def place(plane, rows, first):
             for quad in (0, 2, 1, 3):
-                start = first + 8 * quad
-                nc.sync.dma_start(plane[32 * quad : 32 * quad + 4, :].bitcast(I32), rows[start : start + 7 : 2, :].bitcast(I32))
+                start = first + 16 * quad
+                nc.sync.dma_start(plane[32 * quad : 32 * quad + 4, :].bitcast(I32), rows[start : start + 13 : 4, :].bitcast(I32))
 
-        deal(staged[:, 0:F], weight_rows)
-        deal(dealt_co[:].bitcast(U16), raw_co[:, 0:F].bitcast(U16))
-        nc.vector.tensor_copy(picked_rows[0][:], table_rows[:].indirect(entries(0, HALF)))
-        nc.vector.tensor_copy(staged[:, F:].bitcast(I32), picked_rows[0][:].bitcast(I32))
-        place(first_planes, staged, ROWS)
-        place(second_planes, staged[:, 0:F], ROWS + 1)
-        nc.vector.tensor_copy(picked_rows[1][:], table_rows[:].indirect(entries(HALF, HALF)))
-        late_co = keep.tile([P, F], U8, name="late_co", tag="rows_then_co", align_bytes=64)
-        deal(late_co[:].bitcast(U16), raw_co[:, F:].bitcast(U16))
-        dealt_si = keep.tile([P, 2 * F], U8, name="dealt_si", tag="co_then_si", align_bytes=64)
+        deal(dealt_co[:].bitcast(U16), raw_co[:].bitcast(U16))
         deal(dealt_si[:].bitcast(U16), raw_si[:].bitcast(U16))
-        dealt = ((dealt_co[:], dealt_si[:, 0:F]), (late_co[:], dealt_si[:, F:]))
-        place(late_plane, picked_rows[1], ROWS)
+        nc.vector.tensor_copy(early_rows[:], table_rows[:].indirect(entries(0, HALF)))
+        deal(staged[:, 0:F_PASS], weight_rows[:, 0:F_PASS])
+        deal(staged[:, F_PASS:F], weight_rows[:, F_PASS:])
+        nc.vector.tensor_copy(staged[:, F:].bitcast(I32), early_rows[:].bitcast(I32))
+        place(first_planes, staged, ROWS)
+        place(second_planes, staged[:, 0:F], ROWS + 2)
+        late_rows = keep.tile([P, HALF], U8, name="late_rows", tag="rows_then_picked", align_bytes=64)
+        nc.vector.tensor_copy(late_rows[:], table_rows[:].indirect(entries(HALF, HALF)))
+        place(late_plane, late_rows, ROWS)
         for quad in range(4):
             nc.sync.dma_start(
                 fb_plane[32 * quad : 32 * quad + 4, :, :].bitcast(I32),
@@ -133,10 +129,10 @@ def tile_list_meltab_root_kernel(
         for warm in range(4):
             nc.tensor.matmul_mx(
                 unread[:],
-                lhsT=late_co[:, 0 : 2 * P].bitcast(FP4X4),
-                lhsT_scale=weight_rows[:, 0:P],
-                rhs=rows[:, 0 : PACK * BANK].bitcast(FP8X4),
-                rhs_scale=weight_rows[:, 0:BANK],
+                lhsT=staged[:, 0 : PACK * P].bitcast(FP8X4),
+                lhsT_scale=staged[:, 0:P],
+                rhs=dealt_si[:, 0 : 2 * BANK].bitcast(FP4X4),
+                rhs_scale=staged[:, 0:BANK],
                 start=True,
                 stop=True,
             )
@@ -144,132 +140,130 @@ def tile_list_meltab_root_kernel(
         for g, (j0, width) in enumerate(GATHERS):
             nc.vector.tensor_copy(picked[g][:], table[:].bitcast(U32).indirect(entries(j0, width)))
 
-        def fill(place_in, u, t0, per_bank, first, width):
-            j0, b = UNITS[u][0] + first, UNITS[u][2]
+        def fill(place_in, b, slices, j0, width):
             h, c0 = divmod(j0, HALF)
             g = max(i for i, (g0, g_width) in enumerate(GATHERS) if g0 <= j0)
             g0 = j0 - GATHERS[g][0]
-            bank = psum.tile([P, per_bank, 2, width], F32, name="bank", tag=f"bank{place_in}")
-            for t in range(t0, t0 + per_bank):
-                for part in range(2):
+            bank = psum.tile([P, len(slices), 2, width], F32, name="bank", tag=f"bank{place_in}")
+            for i, t in enumerate(slices):
+                s = b * PACK + t
+                for part, dealt in enumerate((dealt_co, dealt_si)):
                     nc.tensor.matmul_mx(
-                        bank[:, t - t0, part, :],
-                        lhsT=dealt[b][part][:, 2 * P * t : 2 * P * (t + 1)].bitcast(FP4X4),
+                        bank[:, i, part, :],
+                        lhsT=dealt[:, 2 * P * s : 2 * P * (s + 1)].bitcast(FP4X4),
                         lhsT_scale=weight_planes[b][:, part * F_PASS + P * t : part * F_PASS + P * (t + 1)],
                         rhs=picked[g][:, g0 : g0 + width].bitcast(FP8X4),
                         rhs_scale=picked_planes[h][:, c0 : c0 + width],
                         start=True,
                         stop=True,
                     )
-            return [bank[:, i, :, :] for i in range(per_bank)]
+            return bank
 
-        squares = [keep.tile([P, PACK, 2, width], F32, name=f"squares{u}", align_bytes=64) for u, (j0, width, b) in enumerate(UNITS)]
-
+        squares = [keep.tile([P, PACK, 2, width], F32, name=f"squares{u}") for u, (j0, width, b) in enumerate(UNITS)]
+        wovens = [keep.tile([P, PACK * width], BF16, name=f"woven{u}", align_bytes=64) for u, (j0, width, b) in enumerate(UNITS)]
         scalar_banks = [i % 4 for i in range(15)] + [6, 7] + [i % 4 for i in range(15, 25)]
         vector_banks = [4, 5, 6, 7, 4, 5]
         sum_banks = [6, 7, 4, 5, 6]
 
-        def square_on_scalar(u, t0, per_bank, first, width):
-            for i, bank in enumerate(fill(scalar_banks.pop(0), u, t0, per_bank, first, width)):
-                t = t0 + i
-                nc.scalar.activation(squares[u][:, t, :, first : first + width], bank, SQUARE, scale=root_gain[:, UNITS[u][2], t : t + 1])
+        def square_on_scalar(u, slices, first, width):
+            j0, b = UNITS[u][0], UNITS[u][2]
+            bank = fill(scalar_banks.pop(0), b, slices, j0 + first, width)
+            for i, t in enumerate(slices):
+                nc.scalar.activation(squares[u][:, t, :, first : first + width], bank[:, i, :, :], SQUARE, scale=root_gain[:, b, t : t + 1])
 
-        def power(engine, u, woven, first, width):
+        def squares_of(u):
+            width = UNITS[u][1]
+            per_bank = BANK // (2 * width)
+            for t0 in range(0, PACK, per_bank):
+                square_on_scalar(u, range(t0, t0 + per_bank), 0, width)
+
+        def square_on_vector(u, slices, first):
+            j0, b = UNITS[u][0], UNITS[u][2]
+            pending = []
+            for t in slices:
+                bank = fill(vector_banks.pop(0), b, (t,), j0 + first, WIDE)[:, 0, :, :]
+                if vector_banks:
+                    copied = work.tile([P, 2, WIDE], F32, name="copied")
+                else:
+                    copied = keep.tile([P, 2, WIDE], F32, name="last_copied", tag="copied_then_plane", align_bytes=64)
+                nc.vector.tensor_copy(copied[:], bank)
+                pending.append((squares[u][:, t, :, first : first + WIDE], bank, gain[:, b, t : t + 1], copied[:]))
+            for operands in pending:
+                nc.vector.scalar_tensor_tensor(*operands, MULT, MULT)
+
+        def power(engine, u, first, width):
             engine.tensor_tensor(
-                woven.rearrange("p (c i t) -> p c t i", i=RUN, t=PACK),
+                wovens[u][:, PACK * first : PACK * (first + width)].rearrange("p (c i t) -> p c t i", i=RUN, t=PACK),
                 squares[u][:, :, 0, first : first + width].rearrange("p t (c i) -> p c t i", i=RUN),
                 squares[u][:, :, 1, first : first + width].rearrange("p t (c i) -> p c t i", i=RUN),
                 ADD,
             )
 
         sums = {}
-        chunks = [(j0, width) for j0, width, b in UNITS if b == PASSES - 1]
 
-        def second_stage(u, woven, plane, first=0, columns=None):
-            b = UNITS[u][2]
-            u0, u_width = UNITS[u][0] + first, columns or UNITS[u][1]
-            codes = work.tile([P, u_width], U32, name="codes", align_bytes=64, bufs=5)
-            nc.vector.quantize_mx(codes[:].bitcast(FP8X4), plane[:], woven[:])
-            for j0, width in chunks:
-                lo, hi = max(j0, u0), min(j0 + width, u0 + u_width)
-                if lo < hi:
+        def second_stage(u, plane):
+            u0, u_width, b = UNITS[u]
+            codes = keep.tile([P, u_width], U32, name=f"codes{u}", align_bytes=64)
+            nc.vector.quantize_mx(codes[:].bitcast(FP8X4), plane[:], wovens[u][:])
+            for j0, width, blocks in CHUNKS:
+                if u0 <= j0 < u0 + u_width:
                     if b == 0:
-                        sums[j0] = psum.tile([P, N // P, width], F32, name="sums", tag=f"bank{sum_banks.pop(0)}")
-                    for a in range(N // P):
+                        sums[j0, blocks] = psum.tile([P, len(blocks), width], F32, name="sums", tag=f"bank{sum_banks.pop(0)}")
+                    for i, a in enumerate(blocks):
                         nc.tensor.matmul_mx(
-                            sums[j0][:, a, lo - j0 : hi - j0],
+                            sums[j0, blocks][:, i, :],
                             lhsT=fb_codes[:, b, 2 * P * a : 2 * P * (a + 1)].bitcast(FP4X4),
                             lhsT_scale=fb_plane[:, b, P * a : P * (a + 1)],
-                            rhs=codes[:, lo - u0 : hi - u0].bitcast(FP8X4),
-                            rhs_scale=plane[:, lo - u0 : hi - u0],
-                            start=(b == 0 and a == 0),
-                            stop=(b == PASSES - 1 and a == N // P - 1 and hi == j0 + width),
+                            rhs=codes[:, j0 - u0 : j0 - u0 + width].bitcast(FP8X4),
+                            rhs_scale=plane[:, j0 - u0 : j0 - u0 + width],
+                            start=(b == 0 and i == 0),
+                            stop=(b == PASSES - 1 and i == len(blocks) - 1),
                         )
 
-        def finish(u):
-            j0, width, b = UNITS[u]
-            if b == PASSES - 1:
-                result = work.tile([P, N // P, width], F32, name="result", bufs=5)
-                nc.scalar.activation(result[:].rearrange("p a c -> p (a c)"), sums[j0][:].rearrange("p a c -> p (a c)"), SQRT)
-                nc.sync.dma_start(out.rearrange("(a p) j -> p a j", p=P)[:, :, j0 : j0 + width], result[:])
+        def own_plane(u):
+            return keep.tile([P, UNITS[u][1]], U8, name=f"plane{u}", align_bytes=64)
 
-        groups = (((1, 2, WIDE), (1, 3, WIDE)), ((2, 0, WIDE), (2, 1, WIDE)), ((2, 2, WIDE), (2, 3, WIDE)))
-        on_scalar = [(0, 0, 1, 0, P), (0, 1, 1, 0, P), (0, 2, 2, 0, P), (0, 0, 2, P, P), (0, 2, 2, P, P)] + [(1, t, 1, 0, WIDE) for t in (0, 1)]
-        on_scalar = on_scalar + [(u, t, 1, 0, WIDE) for u in (3, 4) for t in range(PACK)]
-        wovens = {u: keep.tile([P, PACK * columns], BF16, name=f"pool_woven{u}", align_bytes=64) for u, columns in ((0, WIDE), (1, WIDE), (3, POOL_PART))}
-        for i, (u, t, per_bank, first, width) in enumerate(on_scalar):
-            square_on_scalar(u, t, per_bank, first, width)
-            if u == 0 and t == 2:
-                power(nc.gpsimd, u, wovens[u][:, PACK * first : PACK * (first + width)], first, width)
-            if (u, t) == (1, 1):
-                power(nc.gpsimd, u, wovens[u][:], 0, WIDE)
-            if (u, t) == (3, 3):
-                power(nc.gpsimd, u, wovens[u][:], 0, POOL_PART)
-            if i % 4 == 3 and i // 4 < len(groups):
-                pending = []
-                for vu, vt, columns in groups[i // 4]:
-                    bank = fill(vector_banks.pop(0), vu, vt, 1, 0, columns)[0]
-                    if (vu, vt) == (2, 3):
-                        copied = turn.tile([P, 2, columns], F32, name="last_copied", offset=0)
-                    else:
-                        copied = work.tile([P, 2, columns], F32, name="copied")
-                    nc.vector.tensor_copy(copied[:], bank)
-                    pending.append((squares[vu][:, vt, :, 0:columns], bank, gain[:, UNITS[vu][2], vt : vt + 1], copied[:]))
-                for operands in pending:
-                    nc.vector.scalar_tensor_tensor(*operands, MULT, MULT)
+        def finish(chunk):
+            j0, width, blocks = CHUNKS[chunk]
+            result = keep.tile([P, len(blocks), width], F32, name=f"result{chunk}")
+            nc.scalar.activation(result[:].rearrange("p a c -> p (a c)"), sums[j0, blocks][:].rearrange("p a c -> p (a c)"), SQRT)
+            nc.sync.dma_start(out.rearrange("(a p) j -> p a j", p=P)[:, blocks[0] : blocks[-1] + 1, j0 : j0 + width], result[:])
 
-        def add_on_vector(u):
-            wovens[u] = work.tile([P, UNITS[u][1] * PACK], BF16, name="woven", align_bytes=64)
-            power(nc.vector, u, wovens[u][:], 0, UNITS[u][1])
-
-        def squares_of(u):
-            per_bank = BANK // (2 * UNITS[u][1])
-            for t0 in range(0, PACK, per_bank):
-                square_on_scalar(u, t0, per_bank, 0, UNITS[u][1])
-
-        def plane_of(u):
-            if u < 2:
-                return turn.tile([P, WIDE], U8, name=f"plane{u}", offset=WIDE * u, align_bytes=64)
-            return work.tile([P, UNITS[u][1]], U8, name="plane", align_bytes=64, bufs=5)
-
-        squares_of(5)
-        second_stage(0, wovens[0], plane_of(0))
-        add_on_vector(2)
-        second_stage(1, wovens[1], plane_of(1))
-        rest = turn.tile([P, PACK * (WIDE - POOL_PART)], BF16, name="rest", offset=2 * WIDE, align_bytes=64)
-        power(nc.vector, 3, rest[:], POOL_PART, WIDE - POOL_PART)
-        second_stage(2, wovens[2], plane_of(2))
-        second_stage(3, wovens[3], keep.tile([P, POOL_PART], U8, name="pool_plane", tag="squares3", align_bytes=64), 0, POOL_PART)
-        second_stage(3, rest, plane_of(7), POOL_PART, WIDE - POOL_PART)
+        square_on_scalar(0, (0,), 0, P)
+        square_on_scalar(0, (1,), 0, P)
+        square_on_scalar(0, (2, 3), 0, P)
+        power(nc.gpsimd, 0, 0, P)
+        square_on_scalar(0, (0, 1), P, P)
+        square_on_vector(0, (2, 3), WIDE)
+        square_on_scalar(0, (2, 3), P, P)
+        power(nc.gpsimd, 0, P, P)
+        square_on_scalar(0, (0,), WIDE, WIDE)
+        square_on_scalar(0, (1,), WIDE, WIDE)
+        power(nc.gpsimd, 0, WIDE, WIDE)
+        square_on_scalar(1, (0,), WIDE, WIDE)
+        square_on_vector(1, (0, 1), 0)
+        for t in (1, 2, 3):
+            square_on_scalar(1, (t,), WIDE, WIDE)
+        power(nc.gpsimd, 1, HALF - POOL_PART, POOL_PART)
+        square_on_scalar(2, (0,), 0, WIDE)
+        square_on_vector(1, (2, 3), 0)
+        for t in (1, 2, 3):
+            square_on_scalar(2, (t,), 0, WIDE)
+        squares_of(3)
+        power(nc.vector, 1, 0, HALF - POOL_PART)
+        second_stage(0, keep.tile([P, HALF], U8, name="held_plane", tag="copied_then_plane", align_bytes=64))
+        second_stage(1, own_plane(1))
         count = len(UNITS)
-        for u in range(4, count + 3):
+        for u in range(2, count + 1):
             if u + 2 < count:
                 squares_of(u + 2)
             if u < count:
-                add_on_vector(u)
-            if 4 <= u - 1 < count:
-                second_stage(u - 1, wovens[u - 1], plane_of(u - 1))
-            if u == 6:
-                finish(3)
-            elif u != 5 and u - 2 < count:
-                finish(u - 2)
+                power(nc.vector, u, 0, UNITS[u][1])
+            if u > 2:
+                second_stage(u - 1, own_plane(u - 1))
+            if u == 2:
+                finish(0)
+            if u == 4:
+                finish(1)
+        for chunk in range(2, len(CHUNKS)):
+            finish(chunk)

@@ -34,7 +34,7 @@ UNITS = (
     (768, 128, 1),
     (896, 128, 1),
 )
-CHUNKS = ((0, 512, (0,)), (0, 512, (1,)), (512, 256, (0, 1)), (768, 128, (0, 1)), (896, 128, (0, 1)))
+CHUNKS = ((0, 512, (0,)), (0, 512, (1,)), (512, 256, (0, 1)), (768, 128, (0, 1)), (896, 128, (0,)), (896, 128, (1,)))
 GATHERS = ((0, 256), (256, 256), (512, 512))
 POOL_PART = 128
 RUN = 4
@@ -161,9 +161,9 @@ def tile_list_meltab_root_kernel(
 
         squares = [keep.tile([P, PACK, 2, width], F32, name=f"squares{u}") for u, (j0, width, b) in enumerate(UNITS)]
         wovens = [keep.tile([P, PACK * width], BF16, name=f"woven{u}", align_bytes=64) for u, (j0, width, b) in enumerate(UNITS)]
-        scalar_banks = [i % 4 for i in range(15)] + [6, 7] + [i % 4 for i in range(15, 25)]
+        scalar_banks = [i % 4 for i in range(18)] + [6, 7] + [(2, 3, 0)[i % 3] for i in range(7)]
         vector_banks = [4, 5, 6, 7, 4, 5]
-        sum_banks = [6, 7, 4, 5, 6]
+        sum_banks = [6, 7, 4, 5, 6, 1]
 
         def square_on_scalar(u, slices, first, width):
             j0, b = UNITS[u][0], UNITS[u][2]
@@ -250,12 +250,13 @@ def tile_list_meltab_root_kernel(
         for t in (1, 2, 3):
             square_on_scalar(2, (t,), 0, WIDE)
         squares_of(3)
+        squares_of(4)
         power(nc.vector, 1, 0, HALF - POOL_PART)
         second_stage(0, keep.tile([P, HALF], U8, name="held_plane", tag="copied_then_plane", align_bytes=64))
         second_stage(1, own_plane(1))
         count = len(UNITS)
         for u in range(2, count + 1):
-            if u + 2 < count:
+            if 4 < u + 2 < count:
                 squares_of(u + 2)
             if u < count:
                 power(nc.vector, u, 0, UNITS[u][1])

@@ -161,9 +161,9 @@ def tile_list_meltab_root_kernel(
 
         squares = [keep.tile([P, PACK, 2, width], F32, name=f"squares{u}") for u, (j0, width, b) in enumerate(UNITS)]
         wovens = [keep.tile([P, PACK * width], BF16, name=f"woven{u}", align_bytes=64) for u, (j0, width, b) in enumerate(UNITS)]
-        scalar_banks = [i % 4 for i in range(18)] + [6, 7] + [(2, 3, 0)[i % 3] for i in range(7)]
+        scalar_banks = [i % 4 for i in range(18)] + [6, 7] + [i % 4 for i in range(18, 25)]
         vector_banks = [4, 5, 6, 7, 4, 5]
-        sum_banks = [6, 7, 4, 5, 6, 1]
+        sum_banks = [6, 7, 2, 3, 4, 5]
 
         def square_on_scalar(u, slices, first, width):
             j0, b = UNITS[u][0], UNITS[u][2]

@@ -31,8 +31,7 @@ UNITS = (
     (512, 256, 0),
     (512, 256, 1),
     (768, 256, 0),
-    (768, 128, 1),
-    (896, 128, 1),
+    (768, 256, 1),
 )
 CHUNKS = ((0, 512, (0,)), (0, 512, (1,)), (512, 256, (0, 1)), (768, 128, (0, 1)), (896, 128, (0,)), (896, 128, (1,)))
 GATHERS = ((0, 256), (256, 256), (512, 512))
@@ -69,9 +68,9 @@ def tile_list_meltab_root_kernel(
         gain = keep.tile([P, PASSES, PACK], F32, name="gain")
         root_gain = keep.tile([P, PASSES, PACK], F32, name="root_gain")
 
-        nc.vector.memset(weight_rows[:].bitcast(I32), 0)
         nc.vector.memset(table_rows[:, 0 : T // 2].bitcast(I32), 0)
         nc.gpsimd.memset(table_rows[:, T // 2 :].bitcast(I32), 0)
+        nc.vector.memset(weight_rows[:].bitcast(I32), 0)
         nc.vector.memset(first_planes[:].bitcast(I32), 0)
         nc.vector.memset(second_planes[:].bitcast(I32), 0)
         nc.vector.memset(late_plane[:].bitcast(I32), 0)
@@ -80,7 +79,6 @@ def tile_list_meltab_root_kernel(
         nc.sync.dma_start(raw_co[:].bitcast(I32), co_words[0].bitcast(I32))
         nc.sync.dma_start(offsets[:], offs)
         nc.sync.dma_start(raw_si[:].bitcast(I32), si_words[0].bitcast(I32))
-        nc.scalar.dma_start(gain[:], gn.rearrange("(b p t) -> p b t", b=PASSES, t=PACK))
         nc.sync.dma_start(table_rows[ROWS : ROWS + 61 : 4, :].bitcast(I32), tab_scales[0].bitcast(I32))
         for part, scales in enumerate((co_scales, si_scales)):
             nc.sync.dma_start(
@@ -88,6 +86,7 @@ def tile_list_meltab_root_kernel(
                 scales[0].rearrange("q (b f) -> (q b) f", b=PASSES).bitcast(I32),
             )
         nc.sync.dma_start(table[:], tab_words[0].rearrange("p t i -> p (t i)").bitcast(I32))
+        nc.sync.dma_start(gain[:], gn.rearrange("(b p t) -> p b t", b=PASSES, t=PACK))
 
         nc.scalar.activation(root_gain[:], gain[:], SQRT)
 
@@ -201,10 +200,10 @@ def tile_list_meltab_root_kernel(
 
         sums = {}
 
-        def second_stage(u, plane):
-            u0, u_width, b = UNITS[u]
-            codes = keep.tile([P, u_width], U32, name=f"codes{u}", align_bytes=64)
-            nc.vector.quantize_mx(codes[:].bitcast(FP8X4), plane[:], wovens[u][:])
+        def second_stage(u, plane, first, u_width):
+            u0, b = UNITS[u][0] + first, UNITS[u][2]
+            codes = keep.tile([P, u_width], U32, name=f"codes{u}_{first}", align_bytes=64)
+            nc.vector.quantize_mx(codes[:].bitcast(FP8X4), plane[:], wovens[u][:, PACK * first : PACK * (first + u_width)])
             for j0, width, blocks in CHUNKS:
                 if u0 <= j0 < u0 + u_width:
                     if b == 0:
@@ -220,8 +219,8 @@ def tile_list_meltab_root_kernel(
                             stop=(b == PASSES - 1 and i == len(blocks) - 1),
                         )
 
-        def own_plane(u):
-            return keep.tile([P, UNITS[u][1]], U8, name=f"plane{u}", align_bytes=64)
+        def own_plane(u, first, width):
+            return keep.tile([P, width], U8, name=f"plane{u}_{first}", align_bytes=64)
 
         def finish(chunk):
             j0, width, blocks = CHUNKS[chunk]
@@ -252,19 +251,18 @@ def tile_list_meltab_root_kernel(
         squares_of(3)
         squares_of(4)
         power(nc.vector, 1, 0, HALF - POOL_PART)
-        second_stage(0, keep.tile([P, HALF], U8, name="held_plane", tag="copied_then_plane", align_bytes=64))
-        second_stage(1, own_plane(1))
-        count = len(UNITS)
-        for u in range(2, count + 1):
-            if 4 < u + 2 < count:
-                squares_of(u + 2)
-            if u < count:
-                power(nc.vector, u, 0, UNITS[u][1])
-            if u > 2:
-                second_stage(u - 1, own_plane(u - 1))
-            if u == 2:
-                finish(0)
-            if u == 4:
-                finish(1)
-        for chunk in range(2, len(CHUNKS)):
+        second_stage(0, keep.tile([P, HALF], U8, name="held_plane", tag="copied_then_plane", align_bytes=64), 0, HALF)
+        second_stage(1, own_plane(1, 0, HALF), 0, HALF)
+        finish(0)
+        square_on_scalar(5, (0,), 0, WIDE)
+        square_on_scalar(5, (1,), 0, WIDE)
+        square_on_scalar(5, (2, 3), 0, P)
+        square_on_scalar(5, (2, 3), P, P)
+        pieces = ((2, 0, WIDE), (3, 0, WIDE), (4, 0, WIDE), (5, 0, P), (5, P, P))
+        for i, (u, first, width) in enumerate(pieces):
+            power(nc.vector, u, first, width)
+            if i > 0:
+                second_stage(pieces[i - 1][0], own_plane(*pieces[i - 1]), *pieces[i - 1][1:])
+        second_stage(pieces[-1][0], own_plane(*pieces[-1]), *pieces[-1][1:])
+        for chunk in range(1, len(CHUNKS)):
             finish(chunk)

@@ -50,21 +50,21 @@ def tile_list_meltab_root_kernel(
         psum = ctx.enter_context(tc.psum_pool(name="psum", bufs=1))
 
         offsets = keep.tile([P, J // 16], U16, name="offsets")
-        table = keep.tile([P, T], I32, name="table", align_bytes=64)
-        table_rows = keep.tile([P, T], U8, name="table_rows", align_bytes=64)
-        weight_rows = keep.tile([P, F], U8, name="weight_rows", tag="rows_then_picked", align_bytes=64)
-        staged = keep.tile([P, F + HALF], U8, name="staged", align_bytes=64)
-        raw_co = keep.tile([P, 2 * F], U8, name="raw_co", align_bytes=64)
-        raw_si = keep.tile([P, 2 * F], U8, name="raw_si", align_bytes=64)
-        dealt_co = keep.tile([P, 2 * F], U8, name="dealt_co", align_bytes=64)
-        early_rows = keep.tile([P, HALF], U8, name="early_rows", align_bytes=64)
-        dealt_si = keep.tile([P, 2 * F], U8, name="dealt_si", align_bytes=64)
-        picked = [keep.tile([P, width], U32, name=f"picked{g}", align_bytes=64) for g, (j0, width) in enumerate(GATHERS)]
-        first_planes = keep.tile([P, F + HALF], U8, name="first_planes", align_bytes=64)
-        second_planes = keep.tile([P, F], U8, name="second_planes", align_bytes=64)
-        late_plane = keep.tile([P, HALF], U8, name="late_plane", align_bytes=64)
-        fb_plane = keep.tile([P, PASSES, N], U8, name="fb_plane", align_bytes=64)
-        fb_codes = keep.tile([P, PASSES, 2 * N], U8, name="fb_codes", align_bytes=64)
+        table = keep.tile([P, T], I32, name="table", align_bytes=256)
+        table_rows = keep.tile([P, T], U8, name="table_rows", align_bytes=256)
+        weight_rows = keep.tile([P, F], U8, name="weight_rows", tag="rows_then_picked", align_bytes=256)
+        staged = keep.tile([P, F + HALF], U8, name="staged", align_bytes=256)
+        raw_co = keep.tile([P, 2 * F], U8, name="raw_co", align_bytes=256)
+        raw_si = keep.tile([P, 2 * F], U8, name="raw_si", align_bytes=256)
+        dealt_co = keep.tile([P, 2 * F], U8, name="dealt_co", align_bytes=256)
+        early_rows = keep.tile([P, HALF], U8, name="early_rows", align_bytes=256)
+        dealt_si = keep.tile([P, 2 * F], U8, name="dealt_si", align_bytes=256)
+        picked = [keep.tile([P, width], U32, name=f"picked{g}", align_bytes=256) for g, (j0, width) in enumerate(GATHERS)]
+        first_planes = keep.tile([P, F + HALF], U8, name="first_planes", align_bytes=256)
+        second_planes = keep.tile([P, F], U8, name="second_planes", align_bytes=256)
+        late_plane = keep.tile([P, HALF], U8, name="late_plane", align_bytes=256)
+        fb_plane = keep.tile([P, PASSES, N], U8, name="fb_plane", align_bytes=256)
+        fb_codes = keep.tile([P, PASSES, 2 * N], U8, name="fb_codes", align_bytes=256)
         gain = keep.tile([P, PASSES, PACK], F32, name="gain")
         root_gain = keep.tile([P, PASSES, PACK], F32, name="root_gain")
 
@@ -112,7 +112,7 @@ def tile_list_meltab_root_kernel(
         nc.vector.tensor_copy(staged[:, F:].bitcast(I32), early_rows[:].bitcast(I32))
         place(first_planes, staged, ROWS)
         place(second_planes, staged[:, 0:F], ROWS + 2)
-        late_rows = keep.tile([P, HALF], U8, name="late_rows", tag="rows_then_picked", align_bytes=64)
+        late_rows = keep.tile([P, HALF], U8, name="late_rows", tag="rows_then_picked", align_bytes=256)
         nc.vector.tensor_copy(late_rows[:], table_rows[:].indirect(entries(HALF, HALF)))
         place(late_plane, late_rows, ROWS)
         for quad in range(4):
@@ -159,7 +159,7 @@ def tile_list_meltab_root_kernel(
             return bank
 
         squares = [keep.tile([P, PACK, 2, width], F32, name=f"squares{u}") for u, (j0, width, b) in enumerate(UNITS)]
-        wovens = [keep.tile([P, PACK * width], BF16, name=f"woven{u}", align_bytes=64) for u, (j0, width, b) in enumerate(UNITS)]
+        wovens = [keep.tile([P, PACK * width], BF16, name=f"woven{u}", align_bytes=256) for u, (j0, width, b) in enumerate(UNITS)]
         scalar_banks = [i % 4 for i in range(18)] + [6, 7] + [i % 4 for i in range(18, 25)]
         vector_banks = [4, 5, 6, 7, 4, 5]
         sum_banks = [6, 7, 2, 3, 4, 5]
@@ -184,7 +184,7 @@ def tile_list_meltab_root_kernel(
                 if vector_banks:
                     copied = work.tile([P, 2, WIDE], F32, name="copied")
                 else:
-                    copied = keep.tile([P, 2, WIDE], F32, name="last_copied", tag="copied_then_plane", align_bytes=64)
+                    copied = keep.tile([P, 2, WIDE], F32, name="last_copied", tag="copied_then_plane", align_bytes=256)
                 nc.vector.tensor_copy(copied[:], bank)
                 pending.append((squares[u][:, t, :, first : first + WIDE], bank, gain[:, b, t : t + 1], copied[:]))
             for operands in pending:
@@ -202,7 +202,7 @@ def tile_list_meltab_root_kernel(
 
         def second_stage(u, plane, first, u_width):
             u0, b = UNITS[u][0] + first, UNITS[u][2]
-            codes = keep.tile([P, u_width], U32, name=f"codes{u}_{first}", align_bytes=64)
+            codes = keep.tile([P, u_width], U32, name=f"codes{u}_{first}", align_bytes=256)
             nc.vector.quantize_mx(codes[:].bitcast(FP8X4), plane[:], wovens[u][:, PACK * first : PACK * (first + u_width)])
             for j0, width, blocks in CHUNKS:
                 if u0 <= j0 < u0 + u_width:
@@ -220,11 +220,11 @@ def tile_list_meltab_root_kernel(
                         )
 
         def own_plane(u, first, width):
-            return keep.tile([P, width], U8, name=f"plane{u}_{first}", align_bytes=64)
+            return keep.tile([P, width], U8, name=f"plane{u}_{first}", align_bytes=256)
 
         def finish(chunk):
             j0, width, blocks = CHUNKS[chunk]
-            result = keep.tile([P, len(blocks), width], F32, name=f"result{chunk}")
+            result = keep.tile([P, len(blocks), width], F32, name=f"result{chunk}", align_bytes=256)
             nc.scalar.activation(result[:].rearrange("p a c -> p (a c)"), sums[j0, blocks][:].rearrange("p a c -> p (a c)"), SQRT)
             nc.sync.dma_start(out.rearrange("(a p) j -> p a j", p=P)[:, blocks[0] : blocks[-1] + 1, j0 : j0 + width], result[:])
 
@@ -251,7 +251,7 @@ def tile_list_meltab_root_kernel(
         squares_of(3)
         squares_of(4)
         power(nc.vector, 1, 0, HALF - POOL_PART)
-        second_stage(0, keep.tile([P, HALF], U8, name="held_plane", tag="copied_then_plane", align_bytes=64), 0, HALF)
+        second_stage(0, keep.tile([P, HALF], U8, name="held_plane", tag="copied_then_plane", align_bytes=256), 0, HALF)
         second_stage(1, own_plane(1, 0, HALF), 0, HALF)
         finish(0)
         square_on_scalar(5, (0,), 0, WIDE)

from contextlib import ExitStack

import concourse.mybir as mybir

K, F, N, T, J = 512, 1024, 256, 4096, 1024
FLOPS = 2 * 2 * K * F * J + 2 * F * N * J

F32 = mybir.dt.float32
BF16 = mybir.dt.bfloat16
I32 = mybir.dt.int32
U32 = mybir.dt.uint32
U16 = mybir.dt.uint16
U8 = mybir.dt.uint8
FP8X4 = mybir.dt.float8_e4m3fn_x4
FP4X4 = mybir.dt.float4_e2m1fn_x4
ADD = mybir.AluOpType.add
MULT = mybir.AluOpType.mult
SQUARE = mybir.ActivationFunctionType.Square
SQRT = mybir.ActivationFunctionType.Sqrt

P = 128
PACK = 4
F_PASS = P * PACK
PASSES = F // F_PASS
BANK = 512
HALF = J // 2
WIDE = 256
UNITS = (
    (0, 512, 0),
    (0, 512, 1),
    (512, 256, 0),
    (512, 256, 1),
    (768, 256, 0),
    (768, 256, 1),
)
CHUNKS = ((0, 512, (0,)), (0, 512, (1,)), (512, 256, (0, 1)), (768, 128, (0, 1)), (896, 128, (0,)), (896, 128, (1,)))
GATHERS = ((0, 256), (256, 256), (512, 512))
POOL_PART = 128
RUN = 4
ROWS = 32


def tile_list_meltab_root_kernel(
    tc, tab_words, tab_scales, co_words, co_scales, si_words, si_scales, gn, fb_words, fb_scales, offs, out
):
    nc = tc.nc
    with ExitStack() as ctx:
        keep = ctx.enter_context(tc.tile_pool(name="keep", bufs=1))
        work = ctx.enter_context(tc.tile_pool(name="work", bufs=3))
        psum = ctx.enter_context(tc.psum_pool(name="psum", bufs=1))

        offsets = keep.tile([P, J // 16], U16, name="offsets")
        table = keep.tile([P, T], I32, name="table", align_bytes=256)
        table_rows = keep.tile([P, T], U8, name="table_rows", align_bytes=256)
        weight_rows = keep.tile([P, F], U8, name="weight_rows", tag="rows_then_picked", align_bytes=256)
        staged = keep.tile([P, F + HALF], U8, name="staged", align_bytes=256)
        raw_co = keep.tile([P, 2 * F], U8, name="raw_co", align_bytes=256)
        raw_si = keep.tile([P, 2 * F], U8, name="raw_si", align_bytes=256)
        dealt_co = keep.tile([P, 2 * F], U8, name="dealt_co", align_bytes=256)
        early_rows = keep.tile([P, HALF], U8, name="early_rows", align_bytes=256)
        dealt_si = keep.tile([P, 2 * F], U8, name="dealt_si", align_bytes=256)
        picked = [keep.tile([P, width], U32, name=f"picked{g}", align_bytes=256) for g, (j0, width) in enumerate(GATHERS)]
        first_planes = keep.tile([P, F + HALF], U8, name="first_planes", align_bytes=256)
        second_planes = keep.tile([P, F], U8, name="second_planes", align_bytes=256)
        late_plane = keep.tile([P, HALF], U8, name="late_plane", align_bytes=256)
        fb_plane = keep.tile([P, PASSES, N], U8, name="fb_plane", align_bytes=256)
        fb_codes = keep.tile([P, PASSES, 2 * N], U8, name="fb_codes", align_bytes=256)
        gain = keep.tile([P, PASSES, PACK], F32, name="gain")
        root_gain = keep.tile([P, PASSES, PACK], F32, name="root_gain")

        nc.vector.memset(table_rows[:, 0 : T // 2].bitcast(I32), 0)
        nc.gpsimd.memset(table_rows[:, T // 2 :].bitcast(I32), 0)
        nc.vector.memset(weight_rows[:].bitcast(I32), 0)
        nc.vector.memset(first_planes[:].bitcast(I32), 0)
        nc.vector.memset(second_planes[:].bitcast(I32), 0)
        nc.vector.memset(late_plane[:].bitcast(I32), 0)
        nc.vector.memset(fb_plane[:].bitcast(I32), 0)

        nc.sync.dma_start(raw_co[:].bitcast(I32), co_words[0].bitcast(I32))
        nc.sync.dma_start(offsets[:], offs)
        nc.sync.dma_start(raw_si[:].bitcast(I32), si_words[0].bitcast(I32))
        nc.sync.dma_start(table_rows[ROWS : ROWS + 61 : 4, :].bitcast(I32), tab_scales[0].bitcast(I32))
        for part, scales in enumerate((co_scales, si_scales)):
            nc.sync.dma_start(
                weight_rows[ROWS : ROWS + 63 : 2, part * F_PASS : (part + 1) * F_PASS].bitcast(I32),
                scales[0].rearrange("q (b f) -> (q b) f", b=PASSES).bitcast(I32),
            )
        nc.sync.dma_start(table[:], tab_words[0].rearrange("p t i -> p (t i)").bitcast(I32))
        nc.sync.dma_start(gain[:], gn.rearrange("(b p t) -> p b t", b=PASSES, t=PACK))

        nc.scalar.activation(root_gain[:], gain[:], SQRT)

        def deal(target, raw):
            nc.vector.tensor_copy(
                target.rearrange("p (g t q) -> p g t q", t=PACK, q=P),
                raw.rearrange("p (g q t) -> p g t q", t=PACK, q=P),
            )

        def entries(j0, width):
            return offsets[:, j0 // 16 : (j0 + width) // 16]

        def place(plane, rows, first):
            for quad in (0, 2, 1, 3):
                start = first + 16 * quad
                nc.sync.dma_start(plane[32 * quad : 32 * quad + 4, :].bitcast(I32), rows[start : start + 13 : 4, :].bitcast(I32))

        deal(dealt_co[:].bitcast(U16), raw_co[:].bitcast(U16))
        deal(dealt_si[:].bitcast(U16), raw_si[:].bitcast(U16))
        nc.vector.tensor_copy(early_rows[:], table_rows[:].indirect(entries(0, HALF)))
        deal(staged[:, 0:F_PASS], weight_rows[:, 0:F_PASS])
        deal(staged[:, F_PASS:F], weight_rows[:, F_PASS:])
        nc.vector.tensor_copy(staged[:, F:].bitcast(I32), early_rows[:].bitcast(I32))
        place(first_planes, staged, ROWS)
        place(second_planes, staged[:, 0:F], ROWS + 2)
        late_rows = keep.tile([P, HALF], U8, name="late_rows", tag="rows_then_picked", align_bytes=256)
        nc.vector.tensor_copy(late_rows[:], table_rows[:].indirect(entries(HALF, HALF)))
        place(late_plane, late_rows, ROWS)
        for quad in range(4):
            nc.sync.dma_start(
                fb_plane[32 * quad : 32 * quad + 4, :, :].bitcast(I32),
                fb_scales[:, 4 * quad : 4 * quad + 4, :].rearrange("b r n -> r b n").bitcast(I32),
            )
        nc.sync.dma_start(fb_codes[:].bitcast(I32), fb_words.rearrange("b p w -> p b w").bitcast(I32))
        weight_planes = (first_planes, second_planes)
        picked_planes = (first_planes[:, F:], late_plane[:])

        unread = psum.tile([P, BANK], F32, name="unread", tag="bank7")
        for warm in range(4):
            nc.tensor.matmul_mx(
                unread[:],
                lhsT=staged[:, 0 : PACK * P].bitcast(FP8X4),
                lhsT_scale=staged[:, 0:P],
                rhs=dealt_si[:, 0 : 2 * BANK].bitcast(FP4X4),
                rhs_scale=staged[:, 0:BANK],
                start=True,
                stop=True,
            )

        for g, (j0, width) in enumerate(GATHERS):
            nc.vector.tensor_copy(picked[g][:], table[:].bitcast(U32).indirect(entries(j0, width)))

        def fill(place_in, b, slices, j0, width):
            h, c0 = divmod(j0, HALF)
            g = max(i for i, (g0, g_width) in enumerate(GATHERS) if g0 <= j0)
            g0 = j0 - GATHERS[g][0]
            bank = psum.tile([P, len(slices), 2, width], F32, name="bank", tag=f"bank{place_in}")
            for i, t in enumerate(slices):
                s = b * PACK + t
                for part, dealt in enumerate((dealt_co, dealt_si)):
                    nc.tensor.matmul_mx(
                        bank[:, i, part, :],
                        lhsT=dealt[:, 2 * P * s : 2 * P * (s + 1)].bitcast(FP4X4),
                        lhsT_scale=weight_planes[b][:, part * F_PASS + P * t : part * F_PASS + P * (t + 1)],
                        rhs=picked[g][:, g0 : g0 + width].bitcast(FP8X4),
                        rhs_scale=picked_planes[h][:, c0 : c0 + width],
                        start=True,
                        stop=True,
                    )
            return bank

        squares = [keep.tile([P, PACK, 2, width], F32, name=f"squares{u}") for u, (j0, width, b) in enumerate(UNITS)]
        wovens = [keep.tile([P, PACK * width], BF16, name=f"woven{u}", align_bytes=256) for u, (j0, width, b) in enumerate(UNITS)]
        scalar_banks = [i % 4 for i in range(18)] + [6, 7] + [i % 4 for i in range(18, 25)]
        vector_banks = [4, 5, 6, 7, 4, 5]
        sum_banks = [6, 7, 2, 3, 4, 5]

        def square_on_scalar(u, slices, first, width):
            j0, b = UNITS[u][0], UNITS[u][2]
            bank = fill(scalar_banks.pop(0), b, slices, j0 + first, width)
            for i, t in enumerate(slices):
                nc.scalar.activation(squares[u][:, t, :, first : first + width], bank[:, i, :, :], SQUARE, scale=root_gain[:, b, t : t + 1])

        def squares_of(u):
            width = UNITS[u][1]
            per_bank = BANK // (2 * width)
            for t0 in range(0, PACK, per_bank):
                square_on_scalar(u, range(t0, t0 + per_bank), 0, width)

        def square_on_vector(u, slices, first):
            j0, b = UNITS[u][0], UNITS[u][2]
            pending = []
            for t in slices:
                bank = fill(vector_banks.pop(0), b, (t,), j0 + first, WIDE)[:, 0, :, :]
                if vector_banks:
                    copied = work.tile([P, 2, WIDE], F32, name="copied")
                else:
                    copied = keep.tile([P, 2, WIDE], F32, name="last_copied", tag="copied_then_plane", align_bytes=256)
                nc.vector.tensor_copy(copied[:], bank)
                pending.append((squares[u][:, t, :, first : first + WIDE], bank, gain[:, b, t : t + 1], copied[:]))
            for operands in pending:
                nc.vector.scalar_tensor_tensor(*operands, MULT, MULT)

        def power(engine, u, first, width):
            engine.tensor_tensor(
                wovens[u][:, PACK * first : PACK * (first + width)].rearrange("p (c i t) -> p c t i", i=RUN, t=PACK),
                squares[u][:, :, 0, first : first + width].rearrange("p t (c i) -> p c t i", i=RUN),
                squares[u][:, :, 1, first : first + width].rearrange("p t (c i) -> p c t i", i=RUN),
                ADD,
            )

        sums = {}

        def second_stage(u, plane, first, u_width):
            u0, b = UNITS[u][0] + first, UNITS[u][2]
            codes = keep.tile([P, u_width], U32, name=f"codes{u}_{first}", align_bytes=256)
            nc.vector.quantize_mx(codes[:].bitcast(FP8X4), plane[:], wovens[u][:, PACK * first : PACK * (first + u_width)])
            for j0, width, blocks in CHUNKS:
                if u0 <= j0 < u0 + u_width:
                    if b == 0:
                        sums[j0, blocks] = psum.tile([P, len(blocks), width], F32, name="sums", tag=f"bank{sum_banks.pop(0)}")
                    for i, a in enumerate(blocks):
                        nc.tensor.matmul_mx(
                            sums[j0, blocks][:, i, :],
                            lhsT=fb_codes[:, b, 2 * P * a : 2 * P * (a + 1)].bitcast(FP4X4),
                            lhsT_scale=fb_plane[:, b, P * a : P * (a + 1)],
                            rhs=codes[:, j0 - u0 : j0 - u0 + width].bitcast(FP8X4),
                            rhs_scale=plane[:, j0 - u0 : j0 - u0 + width],
                            start=(b == 0 and i == 0),
                            stop=(b == PASSES - 1 and i == len(blocks) - 1),
                        )

        def own_plane(u, first, width):
            return keep.tile([P, width], U8, name=f"plane{u}_{first}", align_bytes=256)

        def finish(chunk):
            j0, width, blocks = CHUNKS[chunk]
            result = keep.tile([P, len(blocks), width], F32, name=f"result{chunk}", align_bytes=256)
            nc.scalar.activation(result[:].rearrange("p a c -> p (a c)"), sums[j0, blocks][:].rearrange("p a c -> p (a c)"), SQRT)
            nc.sync.dma_start(out.rearrange("(a p) j -> p a j", p=P)[:, blocks[0] : blocks[-1] + 1, j0 : j0 + width], result[:])

        square_on_scalar(0, (0,), 0, P)
        square_on_scalar(0, (1,), 0, P)
        square_on_scalar(0, (2, 3), 0, P)
        power(nc.gpsimd, 0, 0, P)
        square_on_scalar(0, (0, 1), P, P)
        square_on_vector(0, (2, 3), WIDE)
        square_on_scalar(0, (2, 3), P, P)
        power(nc.gpsimd, 0, P, P)
        square_on_scalar(0, (0,), WIDE, WIDE)
        square_on_scalar(0, (1,), WIDE, WIDE)
        power(nc.gpsimd, 0, WIDE, WIDE)
        square_on_scalar(1, (0,), WIDE, WIDE)
        square_on_vector(1, (0, 1), 0)
        for t in (1, 2, 3):
            square_on_scalar(1, (t,), WIDE, WIDE)
        power(nc.gpsimd, 1, HALF - POOL_PART, POOL_PART)
        square_on_scalar(2, (0,), 0, WIDE)
        square_on_vector(1, (2, 3), 0)
        for t in (1, 2, 3):
            square_on_scalar(2, (t,), 0, WIDE)
        squares_of(3)
        squares_of(4)
        power(nc.vector, 1, 0, HALF - POOL_PART)
        second_stage(0, keep.tile([P, HALF], U8, name="held_plane", tag="copied_then_plane", align_bytes=256), 0, HALF)
        second_stage(1, own_plane(1, 0, HALF), 0, HALF)
        finish(0)
        square_on_scalar(5, (0,), 0, WIDE)
        square_on_scalar(5, (1,), 0, WIDE)
        square_on_scalar(5, (2, 3), 0, P)
        square_on_scalar(5, (2, 3), P, P)
        pieces = ((2, 0, WIDE), (3, 0, WIDE), (4, 0, WIDE), (5, 0, P), (5, P, P))
        for i, (u, first, width) in enumerate(pieces):
            power(nc.vector, u, first, width)
            if i > 0:
                second_stage(pieces[i - 1][0], own_plane(*pieces[i - 1]), *pieces[i - 1][1:])
        second_stage(pieces[-1][0], own_plane(*pieces[-1]), *pieces[-1][1:])
        for chunk in range(1, len(CHUNKS)):
            finish(chunk)
